import numpy as np
import ml_dtypes


def mxq(x, axis, fmt="e4m3"):
    dtype, down = {"e4m3": (ml_dtypes.float8_e4m3fn, 7), "e5m2": (ml_dtypes.float8_e5m2, 14)}[fmt]
    v = np.moveaxis(np.asarray(x, np.float32).astype(ml_dtypes.bfloat16).astype(np.float64), axis, -1)
    blocks = v.reshape(v.shape[:-1] + (-1, 32))
    amax = np.abs(blocks).max(-1, keepdims=True)
    byte = np.maximum(np.where(amax > 0, np.frexp(amax)[1] - 1 + 127, 0) - down, 1)
    scale = np.exp2(byte - 127.0)
    codes = (blocks / scale).astype(np.float32).astype(dtype).astype(np.float64)
    return np.moveaxis((codes * scale).reshape(v.shape), -1, axis)


WIDE = False


def mx_kscale(k):
    if not WIDE:
        return np.ones(k)
    levels = np.array([10, -10, 5, -5, 0])
    if k % 512:
        return np.exp2(np.random.permutation(np.resize(levels, k // 32))).repeat(32)
    a = np.empty((k // 512, 16))
    for p in range(k // 512):
        a[p, :8] = np.random.permutation(np.resize(levels, 8))
        for g in range(8):
            far = levels[np.abs(levels - a[p, g]) >= 10]
            a[p, g + 8] = far[np.random.randint(len(far))]
    return np.exp2(a.ravel()).repeat(32)


def f64(x):
    return np.asarray(x).astype(np.float64)


E2M1 = np.array([0.0, 0.5, 1.0, 1.5, 2.0, 3.0, 4.0, 6.0, -0.0, -0.5, -1.0, -1.5, -2.0, -3.0, -4.0, -6.0])


def pack_weight(w, fmt):
    k, n = w.shape
    w = f64(np.asarray(w, np.float32).astype(ml_dtypes.bfloat16)).reshape(k // 32, 32, n)
    amax = np.abs(w).max(1)
    if fmt == "e4m3":
        byte = np.frexp(amax)[1] - 1 + 127 - 7
    else:
        mant, ex = np.frexp(amax / 6.0)
        byte = np.where(mant > 0.5, ex, ex - 1) + 127
    byte = np.clip(np.where(amax > 0, byte, 1), 1, 254)
    scaled = (w * np.exp2(127.0 - byte)[:, None, :]).reshape(k, n).astype(np.float32)
    by_word = np.ascontiguousarray(scaled.reshape(k // 512, 128, 4, n).transpose(0, 1, 3, 2))
    if fmt == "e4m3":
        words = by_word.astype(ml_dtypes.float8_e4m3fn).view(np.uint8)
    else:
        c = by_word.astype(ml_dtypes.float4_e2m1fn).view(np.uint8) & 0xF
        words = (c[..., 0::2] | (c[..., 1::2] << 4)).reshape(k // 512, 128, 2 * n)
    return np.ascontiguousarray(words), np.ascontiguousarray(byte.astype(np.uint8).reshape(k // 512, 16, n))


def unpack_weight(words, scales, fmt):
    g, _, n = scales.shape
    words = np.ascontiguousarray(words).reshape(g, 128, n, -1)
    if fmt == "e4m3":
        vals = words.view(ml_dtypes.float8_e4m3fn).astype(np.float64)
    else:
        nib = np.empty((g, 128, n, 4), np.uint8)
        nib[..., 0::2] = words & 0xF
        nib[..., 1::2] = words >> 4
        vals = E2M1[nib]
    vals = vals * np.repeat(np.exp2(scales.astype(np.float64) - 127.0), 8, axis=1)[..., None]
    return vals.transpose(0, 1, 3, 2).reshape(g * 512, n)


def silu(v):
    return v / (1.0 + np.exp(-np.maximum(v, -700.0)))


K, M, T = 1024, 1536, 512


def setup_inputs():
    n = np.random.standard_normal
    s = mx_kscale(K)[:, None]
    x = n((K, T)) * s
    x4 = pack_weight(x, "e2m1")
    rest = x - unpack_weight(*x4, "e2m1")
    p_w4 = pack_weight(n((K, M)) / np.sqrt(K) / s, "e2m1")
    return {
        "x4_words": x4[0],
        "x4_scales": x4[1],
        "xr": (rest).astype(np.float32),
        "w4_words": p_w4[0],
        "w4_scales": p_w4[1],
        "b": (0.3 * n(1536)).astype(np.float32),
    }


def reference(x4_words, x4_scales, xr, w4_words, w4_scales, b):
    x4_ = unpack_weight(x4_words, x4_scales, "e2m1")
    xr_ = mxq(f64(xr), 0, "e4m3")
    w4_ = unpack_weight(w4_words, w4_scales, "e2m1")
    y = w4_.T @ x4_ + w4_.T @ xr_
    return silu(y + f64(b)[:, None])

@@ -1,0 +1,196 @@
+from contextlib import ExitStack
+
+import concourse.mybir as mybir
+
+K, M, T = 1024, 1536, 512
+FLOPS = 2 * 2 * K * M * T
+
+F32 = mybir.dt.float32
+BF16 = mybir.dt.bfloat16
+I32 = mybir.dt.int32
+U32 = mybir.dt.uint32
+U8 = mybir.dt.uint8
+FP8X4 = mybir.dt.float8_e4m3fn_x4
+FP4X4 = mybir.dt.float4_e2m1fn_x4
+SILU = mybir.ActivationFunctionType.Silu
+
+P = 128
+PACK = 4
+PASSES = 2
+TILES = M // P
+BANKS = 8
+EARLY = 8
+HALF = T // 2
+LAG = 3
+WARM = 30
+VECTOR_COLS = 160
+
+
+def tile_mix_xres_fm_silu_kernel(tc, x4_words, x4_scales, xr, w4_words, w4_scales, b, out):
+    nc = tc.nc
+    with ExitStack() as ctx:
+        keep = ctx.enter_context(tc.tile_pool(name="keep", bufs=1))
+        psum = ctx.enter_context(tc.psum_pool(name="psum", bufs=1))
+        ctx.enter_context(tc.manual_schedule())
+
+        x_words = [keep.tile([P, 2 * T], U8, align_bytes=256, name="x_words%d" % a) for a in range(PASSES)]
+        x_scales = keep.tile([P, PASSES, T], U8, align_bytes=256)
+        half_early = EARLY // 2
+        we_words = [
+            [keep.tile([P, half_early * 2 * P], U8, align_bytes=256, name="we_words%d_%d" % (a, g)) for g in range(2)]
+            for a in range(PASSES)
+        ]
+        we_scales = keep.tile([P, PASSES, EARLY * P], U8, align_bytes=256)
+        wl_words = keep.tile([P, PASSES, (TILES - EARLY) * 2 * P], U8, align_bytes=256)
+        wl_scales = keep.tile([P, PASSES, (TILES - EARLY) * P], U8, align_bytes=256)
+        warm = keep.tile([P, 1], F32)
+        warm_out = keep.tile([P, 1], F32)
+        zeros = keep.tile([P, P], F32)
+        b_rows = keep.tile([P, 32], F32, align_bytes=64)
+        b_cols = keep.tile([P, 32], F32, align_bytes=64)
+
+        nc.gpsimd.memset(zeros[:], 0.0)
+        nc.vector.memset(x_scales[:].bitcast(I32), 0)
+        nc.vector.memset(we_scales[:].bitcast(I32), 0)
+        nc.vector.memset(b_rows[:], 0.0)
+        nc.vector.memset(warm[:], 0.0)
+        nc.vector.memset(wl_scales[:].bitcast(I32), 0)
+
+        xw = x4_words.bitcast(I32).rearrange("a p n -> p a n")
+        ww = w4_words.bitcast(I32)
+        xs = x4_scales.bitcast(I32).rearrange("a (q r) n -> r q a n", r=4)
+        ws = w4_scales.bitcast(I32).rearrange("a (q r) n -> r q a n", r=4)
+        e_words = EARLY * 2 * P // 4
+        e_scales = EARLY * P // 4
+
+        nc.sync.dma_start(out=x_words[0][:].bitcast(I32), in_=xw[:, 0])
+        nc.scalar.dma_start(out=we_words[0][0][:].bitcast(I32), in_=ww[0, :, 0 : e_words // 2])
+        b_view = b.rearrange("(i q c) -> q i c", q=4, c=32)
+        for q in range(4):
+            nc.gpsimd.dma_start(out=b_rows[32 * q : 32 * q + TILES, :], in_=b_view[q])
+
+        for r in range(4):
+            nc.sync.dma_start(out=x_scales[:].bitcast(I32)[r:P:32], in_=xs[r])
+        for r in range(4):
+            queue = nc.scalar if r < 2 else nc.sync
+            queue.dma_start(out=we_scales[:].bitcast(I32)[r:P:32], in_=ws[r, :, :, 0:e_scales])
+        nc.sync.dma_start(out=we_words[0][1][:].bitcast(I32), in_=ww[0, :, e_words // 2 : e_words])
+        nc.sync.dma_start(out=x_words[1][:].bitcast(I32), in_=xw[:, 1])
+        for g in range(2):
+            nc.sync.dma_start(
+                out=we_words[1][g][:].bitcast(I32), in_=ww[1, :, g * e_words // 2 : (g + 1) * e_words // 2]
+            )
+        nc.scalar.activation(warm_out[:], warm[:], SILU)
+
+        xr_view = xr.rearrange("(a p j) t -> a p j t", p=P, j=PACK)
+        raw = [keep.tile([P, PACK, T], F32, name="raw%d" % a) for a in range(PASSES)]
+        nc.sync.dma_start(out=raw[0][:], in_=xr_view[0])
+        for h in range(2):
+            cols = slice(h * HALF, (h + 1) * HALF)
+            nc.sync.dma_start(out=raw[1][:, :, cols], in_=xr_view[1, :, :, cols])
+        nc.sync.dma_start(out=wl_words[:].bitcast(I32), in_=ww.rearrange("a p n -> p a n")[:, :, e_words:])
+        for r in range(4):
+            nc.sync.dma_start(out=wl_scales[:].bitcast(I32)[r:P:32], in_=ws[r, :, :, e_scales:])
+
+        grouped = [keep.tile([P, T, PACK], BF16, align_bytes=256, name="grouped%d" % a) for a in range(PASSES)]
+        codes = [keep.tile([P, T], U32, align_bytes=256, name="codes%d" % a) for a in range(PASSES)]
+        scales = [keep.tile([P, T], U8, align_bytes=256, name="scales%d" % a) for a in range(PASSES)]
+
+        def interleave(a, h):
+            c0 = h * HALF
+            c1 = c0 + VECTOR_COLS
+            c2 = c0 + HALF
+            nc.vector.tensor_copy(out=grouped[a][:, c0:c1, :], in_=raw[a][:, :, c0:c1].rearrange("p j t -> p t j"))
+            nc.scalar.copy(out=grouped[a][:, c1:c2, :], in_=raw[a][:, :, c1:c2].rearrange("p j t -> p t j"))
+
+        def quantize(a, h):
+            cols = slice(h * HALF, (h + 1) * HALF)
+            nc.vector.quantize_mx(
+                out=codes[a][:, cols].bitcast(FP8X4),
+                scales=scales[a][:, cols],
+                in_=grouped[a][:, cols, :].rearrange("p t j -> p (t j)"),
+            )
+
+        interleave(0, 0)
+        interleave(0, 1)
+        quantize(0, 0)
+        quantize(0, 1)
+        interleave(1, 0)
+        quantize(1, 0)
+        interleave(1, 1)
+        quantize(1, 1)
+        nc.vector.transpose(b_cols[:], b_rows[:])
+
+        banks = {}
+        done = {}
+
+        def stationary(i, a):
+            if i < EARLY:
+                g, k = divmod(i, half_early)
+                return (
+                    we_words[a][g][:, 2 * P * k : 2 * P * (k + 1)].bitcast(FP4X4),
+                    we_scales[:, a, P * i : P * (i + 1)],
+                )
+            k = i - EARLY
+            return (
+                wl_words[:, a, 2 * P * k : 2 * P * (k + 1)].bitcast(FP4X4),
+                wl_scales[:, a, P * k : P * (k + 1)],
+            )
+
+        def moving(kind, a, t0, t1):
+            if kind == "x4":
+                return x_words[a][:, 2 * t0 : 2 * t1].bitcast(FP4X4), x_scales[:, a, t0:t1]
+            return codes[a][:, t0:t1].bitcast(FP8X4), scales[a][:, t0:t1]
+
+        def multiply(acc, kind, i, a, t0, t1, start, stop):
+            w_view, w_scale = stationary(i, a)
+            x_view, x_scale = moving(kind, a, t0, t1)
+            nc.tensor.matmul_mx(
+                out=acc, lhsT=w_view, lhsT_scale=w_scale, rhs=x_view, rhs_scale=x_scale, start=start, stop=stop
+            )
+
+        def mx_pass(kind, i, a):
+            if i not in banks:
+                banks[i] = psum.tile([P, T], F32, name="acc%d" % i, tag="bank%d" % (i % BANKS))
+                done[i] = 0
+            multiply(banks[i][:], kind, i, a, 0, T, done[i] == 0, done[i] == 3)
+            done[i] += 1
+            if done[i] == 4:
+                res = keep.tile([P, T], F32, name="res%d" % i)
+                nc.scalar.activation(res[:], banks[i][:], SILU, bias=b_cols[:, i : i + 1])
+                nc.sync.dma_start(out=out[P * i : P * (i + 1), :], in_=res[:])
+
+        def last_tile(i):
+            res = keep.tile([P, T], F32, name="res_last")
+            for n in range(4):
+                t0, t1 = n * P, (n + 1) * P
+                acc = psum.tile([P, P], F32, name="acc_last%d" % n, tag="bank%d" % (3 + n))
+                multiply(acc[:], "x4", i, 0, t0, t1, True, False)
+                multiply(acc[:], "x4", i, 1, t0, t1, False, False)
+                multiply(acc[:], "xr", i, 0, t0, t1, False, False)
+                multiply(acc[:], "xr", i, 1, t0, t1, False, True)
+                nc.scalar.activation(res[:, t0:t1], acc[:], SILU, bias=b_cols[:, i : i + 1])
+                if n == 1:
+                    nc.sync.dma_start(out=out[P * i : P * (i + 1), 0:t1], in_=res[:, 0:t1])
+                if n == 2:
+                    nc.sync.dma_start(out=out[P * i : P * (i + 1), t0:t1], in_=res[:, t0:t1])
+                if n == 3:
+                    nc.scalar.dma_start(out=out[P * i : P * (i + 1), t0:t1], in_=res[:, t0:t1])
+
+        idle = psum.tile([P, P], F32, tag="bank%d" % (BANKS - 1), name="idle")
+        for n in range(WARM):
+            nc.tensor.transpose(idle[:], zeros[:], zeros[:])
+        for a in range(PASSES):
+            for i in range(BANKS):
+                mx_pass("x4", i, a)
+        for i in range(LAG):
+            mx_pass("xr", i, 0)
+        for i in range(BANKS):
+            mx_pass("xr", i, 1)
+            if i + LAG < BANKS:
+                mx_pass("xr", i + LAG, 0)
+        for i in range(BANKS, TILES - 1):
+            for kind in ("x4", "xr"):
+                for a in range(PASSES):
+                    mx_pass(kind, i, a)
+        last_tile(TILES - 1)

@@ -21,8 +21,8 @@ TILES = M // P
 BANKS = 8
 EARLY = 8
 HALF = T // 2
-LAG = 3
-WARM = 30
+LAG = 4
+FIRST = 2
 VECTOR_COLS = 160
 
 
@@ -35,52 +35,43 @@ def tile_mix_xres_fm_silu_kernel(tc, x4_words, x4_scales, xr, w4_words, w4_scale
 
         x_words = [keep.tile([P, 2 * T], U8, align_bytes=256, name="x_words%d" % a) for a in range(PASSES)]
         x_scales = keep.tile([P, PASSES, T], U8, align_bytes=256)
-        half_early = EARLY // 2
-        we_words = [
-            [keep.tile([P, half_early * 2 * P], U8, align_bytes=256, name="we_words%d_%d" % (a, g)) for g in range(2)]
-            for a in range(PASSES)
-        ]
+        wf_words = keep.tile([P, PASSES, FIRST * 2 * P], U8, align_bytes=256)
+        we_words = keep.tile([P, PASSES, (EARLY - FIRST) * 2 * P], U8, align_bytes=256)
         we_scales = keep.tile([P, PASSES, EARLY * P], U8, align_bytes=256)
         wl_words = keep.tile([P, PASSES, (TILES - EARLY) * 2 * P], U8, align_bytes=256)
         wl_scales = keep.tile([P, PASSES, (TILES - EARLY) * P], U8, align_bytes=256)
         warm = keep.tile([P, 1], F32)
         warm_out = keep.tile([P, 1], F32)
-        zeros = keep.tile([P, P], F32)
-        b_rows = keep.tile([P, 32], F32, align_bytes=64)
-        b_cols = keep.tile([P, 32], F32, align_bytes=64)
+        b_rows = keep.tile([P, TILES * 32], F32, align_bytes=64)
+        b_cols = keep.tile([P, TILES * 32], F32, align_bytes=64)
 
-        nc.gpsimd.memset(zeros[:], 0.0)
         nc.vector.memset(x_scales[:].bitcast(I32), 0)
         nc.vector.memset(we_scales[:].bitcast(I32), 0)
-        nc.vector.memset(b_rows[:], 0.0)
         nc.vector.memset(warm[:], 0.0)
+        nc.vector.memset(b_rows[:], 0.0)
         nc.vector.memset(wl_scales[:].bitcast(I32), 0)
 
         xw = x4_words.bitcast(I32).rearrange("a p n -> p a n")
-        ww = w4_words.bitcast(I32)
+        ww = w4_words.bitcast(I32).rearrange("a p n -> p a n")
         xs = x4_scales.bitcast(I32).rearrange("a (q r) n -> r q a n", r=4)
         ws = w4_scales.bitcast(I32).rearrange("a (q r) n -> r q a n", r=4)
+        f_words = FIRST * 2 * P // 4
         e_words = EARLY * 2 * P // 4
         e_scales = EARLY * P // 4
 
         nc.sync.dma_start(out=x_words[0][:].bitcast(I32), in_=xw[:, 0])
-        nc.scalar.dma_start(out=we_words[0][0][:].bitcast(I32), in_=ww[0, :, 0 : e_words // 2])
+        nc.scalar.dma_start(out=wf_words[:].bitcast(I32), in_=ww[:, :, 0:f_words])
+        nc.gpsimd.dma_start(out=we_words[:].bitcast(I32), in_=ww[:, :, f_words:e_words])
+        nc.gpsimd.dma_start(out=x_words[1][:].bitcast(I32), in_=xw[:, 1])
         b_view = b.rearrange("(i q c) -> q i c", q=4, c=32)
-        for q in range(4):
-            nc.gpsimd.dma_start(out=b_rows[32 * q : 32 * q + TILES, :], in_=b_view[q])
 
         for r in range(4):
             nc.sync.dma_start(out=x_scales[:].bitcast(I32)[r:P:32], in_=xs[r])
         for r in range(4):
             queue = nc.scalar if r < 2 else nc.sync
             queue.dma_start(out=we_scales[:].bitcast(I32)[r:P:32], in_=ws[r, :, :, 0:e_scales])
-        nc.sync.dma_start(out=we_words[0][1][:].bitcast(I32), in_=ww[0, :, e_words // 2 : e_words])
-        nc.sync.dma_start(out=x_words[1][:].bitcast(I32), in_=xw[:, 1])
-        for g in range(2):
-            nc.sync.dma_start(
-                out=we_words[1][g][:].bitcast(I32), in_=ww[1, :, g * e_words // 2 : (g + 1) * e_words // 2]
-            )
         nc.scalar.activation(warm_out[:], warm[:], SILU)
+        nc.scalar.dma_start(out=b_rows[0:P:32, :].rearrange("q (i c) -> q i c", c=32), in_=b_view)
 
         xr_view = xr.rearrange("(a p j) t -> a p j t", p=P, j=PACK)
         raw = [keep.tile([P, PACK, T], F32, name="raw%d" % a) for a in range(PASSES)]
@@ -88,7 +79,7 @@ def tile_mix_xres_fm_silu_kernel(tc, x4_words, x4_scales, xr, w4_words, w4_scale
         for h in range(2):
             cols = slice(h * HALF, (h + 1) * HALF)
             nc.sync.dma_start(out=raw[1][:, :, cols], in_=xr_view[1, :, :, cols])
-        nc.sync.dma_start(out=wl_words[:].bitcast(I32), in_=ww.rearrange("a p n -> p a n")[:, :, e_words:])
+        nc.sync.dma_start(out=wl_words[:].bitcast(I32), in_=ww[:, :, e_words:])
         for r in range(4):
             nc.sync.dma_start(out=wl_scales[:].bitcast(I32)[r:P:32], in_=ws[r, :, :, e_scales:])
 
@@ -100,8 +91,14 @@ def tile_mix_xres_fm_silu_kernel(tc, x4_words, x4_scales, xr, w4_words, w4_scale
             c0 = h * HALF
             c1 = c0 + VECTOR_COLS
             c2 = c0 + HALF
-            nc.vector.tensor_copy(out=grouped[a][:, c0:c1, :], in_=raw[a][:, :, c0:c1].rearrange("p j t -> p t j"))
-            nc.scalar.copy(out=grouped[a][:, c1:c2, :], in_=raw[a][:, :, c1:c2].rearrange("p j t -> p t j"))
+            nc.vector.tensor_copy(
+                out=grouped[a][:, c0:c1, :].rearrange("p (c i) j -> p c j i", i=4),
+                in_=raw[a][:, :, c0:c1].rearrange("p j (c i) -> p c j i", i=4),
+            )
+            nc.scalar.copy(
+                out=grouped[a][:, c1:c2, :].rearrange("p (c i) j -> p c j i", i=4),
+                in_=raw[a][:, :, c1:c2].rearrange("p j (c i) -> p c j i", i=4),
+            )
 
         def quantize(a, h):
             cols = slice(h * HALF, (h + 1) * HALF)
@@ -111,6 +108,8 @@ def tile_mix_xres_fm_silu_kernel(tc, x4_words, x4_scales, xr, w4_words, w4_scale
                 in_=grouped[a][:, cols, :].rearrange("p t j -> p (t j)"),
             )
 
+        nc.vector.transpose(b_cols[:, 0:256], b_rows[:, 0:256])
+        nc.vector.transpose(b_cols[:, 256:384], b_rows[:, 256:384])
         interleave(0, 0)
         interleave(0, 1)
         quantize(0, 0)
@@ -119,16 +118,15 @@ def tile_mix_xres_fm_silu_kernel(tc, x4_words, x4_scales, xr, w4_words, w4_scale
         quantize(1, 0)
         interleave(1, 1)
         quantize(1, 1)
-        nc.vector.transpose(b_cols[:], b_rows[:])
 
         banks = {}
         done = {}
 
         def stationary(i, a):
             if i < EARLY:
-                g, k = divmod(i, half_early)
+                words, k = (wf_words, i) if i < FIRST else (we_words, i - FIRST)
                 return (
-                    we_words[a][g][:, 2 * P * k : 2 * P * (k + 1)].bitcast(FP4X4),
+                    words[:, a, 2 * P * k : 2 * P * (k + 1)].bitcast(FP4X4),
                     we_scales[:, a, P * i : P * (i + 1)],
                 )
             k = i - EARLY
@@ -157,7 +155,7 @@ def tile_mix_xres_fm_silu_kernel(tc, x4_words, x4_scales, xr, w4_words, w4_scale
             done[i] += 1
             if done[i] == 4:
                 res = keep.tile([P, T], F32, name="res%d" % i)
-                nc.scalar.activation(res[:], banks[i][:], SILU, bias=b_cols[:, i : i + 1])
+                nc.scalar.activation(res[:], banks[i][:], SILU, bias=b_cols[:, 32 * i : 32 * i + 1])
                 nc.sync.dma_start(out=out[P * i : P * (i + 1), :], in_=res[:])
 
         def last_tile(i):
@@ -169,7 +167,7 @@ def tile_mix_xres_fm_silu_kernel(tc, x4_words, x4_scales, xr, w4_words, w4_scale
                 multiply(acc[:], "x4", i, 1, t0, t1, False, False)
                 multiply(acc[:], "xr", i, 0, t0, t1, False, False)
                 multiply(acc[:], "xr", i, 1, t0, t1, False, True)
-                nc.scalar.activation(res[:, t0:t1], acc[:], SILU, bias=b_cols[:, i : i + 1])
+                nc.scalar.activation(res[:, t0:t1], acc[:], SILU, bias=b_cols[:, 32 * i : 32 * i + 1])
                 if n == 1:
                     nc.sync.dma_start(out=out[P * i : P * (i + 1), 0:t1], in_=res[:, 0:t1])
                 if n == 2:
@@ -177,9 +175,6 @@ def tile_mix_xres_fm_silu_kernel(tc, x4_words, x4_scales, xr, w4_words, w4_scale
                 if n == 3:
                     nc.scalar.dma_start(out=out[P * i : P * (i + 1), t0:t1], in_=res[:, t0:t1])
 
-        idle = psum.tile([P, P], F32, tag="bank%d" % (BANKS - 1), name="idle")
-        for n in range(WARM):
-            nc.tensor.transpose(idle[:], zeros[:], zeros[:])
         for a in range(PASSES):
             for i in range(BANKS):
                 mx_pass("x4", i, a)

@@ -21,9 +21,9 @@ TILES = M // P
 BANKS = 8
 EARLY = 8
 HALF = T // 2
-LAG = 4
-FIRST = 2
-VECTOR_COLS = 160
+LAG = 3
+WARM = (512, 512, 256)
+VECTOR_COLS = 152
 
 
 def tile_mix_xres_fm_silu_kernel(tc, x4_words, x4_scales, xr, w4_words, w4_scales, b, out):
@@ -35,8 +35,7 @@ def tile_mix_xres_fm_silu_kernel(tc, x4_words, x4_scales, xr, w4_words, w4_scale
 
         x_words = [keep.tile([P, 2 * T], U8, align_bytes=256, name="x_words%d" % a) for a in range(PASSES)]
         x_scales = keep.tile([P, PASSES, T], U8, align_bytes=256)
-        wf_words = keep.tile([P, PASSES, FIRST * 2 * P], U8, align_bytes=256)
-        we_words = keep.tile([P, PASSES, (EARLY - FIRST) * 2 * P], U8, align_bytes=256)
+        we_words = keep.tile([P, PASSES, EARLY * 2 * P], U8, align_bytes=256)
         we_scales = keep.tile([P, PASSES, EARLY * P], U8, align_bytes=256)
         wl_words = keep.tile([P, PASSES, (TILES - EARLY) * 2 * P], U8, align_bytes=256)
         wl_scales = keep.tile([P, PASSES, (TILES - EARLY) * P], U8, align_bytes=256)
@@ -55,30 +54,27 @@ def tile_mix_xres_fm_silu_kernel(tc, x4_words, x4_scales, xr, w4_words, w4_scale
         ww = w4_words.bitcast(I32).rearrange("a p n -> p a n")
         xs = x4_scales.bitcast(I32).rearrange("a (q r) n -> r q a n", r=4)
         ws = w4_scales.bitcast(I32).rearrange("a (q r) n -> r q a n", r=4)
-        f_words = FIRST * 2 * P // 4
         e_words = EARLY * 2 * P // 4
         e_scales = EARLY * P // 4
 
         nc.sync.dma_start(out=x_words[0][:].bitcast(I32), in_=xw[:, 0])
-        nc.scalar.dma_start(out=wf_words[:].bitcast(I32), in_=ww[:, :, 0:f_words])
-        nc.gpsimd.dma_start(out=we_words[:].bitcast(I32), in_=ww[:, :, f_words:e_words])
         nc.gpsimd.dma_start(out=x_words[1][:].bitcast(I32), in_=xw[:, 1])
         b_view = b.rearrange("(i q c) -> q i c", q=4, c=32)
 
         for r in range(4):
-            nc.sync.dma_start(out=x_scales[:].bitcast(I32)[r:P:32], in_=xs[r])
-        for r in range(4):
             queue = nc.scalar if r < 2 else nc.sync
+            queue.dma_start(out=x_scales[:].bitcast(I32)[r:P:32], in_=xs[r])
+        nc.scalar.dma_start(out=we_words[:].bitcast(I32), in_=ww[:, :, 0:e_words])
+        for r in range(4):
+            queue = nc.scalar if r == 1 else nc.sync
             queue.dma_start(out=we_scales[:].bitcast(I32)[r:P:32], in_=ws[r, :, :, 0:e_scales])
         nc.scalar.activation(warm_out[:], warm[:], SILU)
-        nc.scalar.dma_start(out=b_rows[0:P:32, :].rearrange("q (i c) -> q i c", c=32), in_=b_view)
+        nc.sync.dma_start(out=b_rows[0:P:32, :].rearrange("q (i c) -> q i c", c=32), in_=b_view)
 
         xr_view = xr.rearrange("(a p j) t -> a p j t", p=P, j=PACK)
         raw = [keep.tile([P, PACK, T], F32, name="raw%d" % a) for a in range(PASSES)]
-        nc.sync.dma_start(out=raw[0][:], in_=xr_view[0])
-        for h in range(2):
-            cols = slice(h * HALF, (h + 1) * HALF)
-            nc.sync.dma_start(out=raw[1][:, :, cols], in_=xr_view[1, :, :, cols])
+        for a in range(PASSES):
+            nc.sync.dma_start(out=raw[a][:], in_=xr_view[a])
         nc.sync.dma_start(out=wl_words[:].bitcast(I32), in_=ww[:, :, e_words:])
         for r in range(4):
             nc.sync.dma_start(out=wl_scales[:].bitcast(I32)[r:P:32], in_=ws[r, :, :, e_scales:])
@@ -110,23 +106,19 @@ def tile_mix_xres_fm_silu_kernel(tc, x4_words, x4_scales, xr, w4_words, w4_scale
 
         nc.vector.transpose(b_cols[:, 0:256], b_rows[:, 0:256])
         nc.vector.transpose(b_cols[:, 256:384], b_rows[:, 256:384])
-        interleave(0, 0)
-        interleave(0, 1)
-        quantize(0, 0)
-        quantize(0, 1)
-        interleave(1, 0)
-        quantize(1, 0)
-        interleave(1, 1)
-        quantize(1, 1)
+        for a in range(PASSES):
+            for h in range(2):
+                interleave(a, h)
+            for h in range(2):
+                quantize(a, h)
 
         banks = {}
         done = {}
 
         def stationary(i, a):
             if i < EARLY:
-                words, k = (wf_words, i) if i < FIRST else (we_words, i - FIRST)
                 return (
-                    words[:, a, 2 * P * k : 2 * P * (k + 1)].bitcast(FP4X4),
+                    we_words[:, a, 2 * P * i : 2 * P * (i + 1)].bitcast(FP4X4),
                     we_scales[:, a, P * i : P * (i + 1)],
                 )
             k = i - EARLY
@@ -175,6 +167,19 @@ def tile_mix_xres_fm_silu_kernel(tc, x4_words, x4_scales, xr, w4_words, w4_scale
                 if n == 3:
                     nc.scalar.dma_start(out=out[P * i : P * (i + 1), t0:t1], in_=res[:, t0:t1])
 
+        idle = psum.tile([P, T], F32, tag="bank%d" % (BANKS - 1), name="idle")
+        for n, width in enumerate(WARM):
+            x_view, x_scale = moving("x4", 0, 0, width)
+            s_view, s_scale = moving("x4", 0, 0, P)
+            nc.tensor.matmul_mx(
+                out=idle[:, 0:width],
+                lhsT=s_view,
+                lhsT_scale=s_scale,
+                rhs=x_view,
+                rhs_scale=x_scale,
+                start=n == 0,
+                stop=n == len(WARM) - 1,
+            )
         for a in range(PASSES):
             for i in range(BANKS):
                 mx_pass("x4", i, a)

@@ -21,7 +21,8 @@ TILES = M // P
 BANKS = 8
 EARLY = 8
 HALF = T // 2
-LAG = 3
+LAG = 2
+LAST = ((0, 256), (256, 384), (384, 512))
 WARM = (512, 512, 256)
 VECTOR_COLS = 152
 
@@ -69,12 +70,12 @@ def tile_mix_xres_fm_silu_kernel(tc, x4_words, x4_scales, xr, w4_words, w4_scale
             queue = nc.scalar if r == 1 else nc.sync
             queue.dma_start(out=we_scales[:].bitcast(I32)[r:P:32], in_=ws[r, :, :, 0:e_scales])
         nc.scalar.activation(warm_out[:], warm[:], SILU)
-        nc.sync.dma_start(out=b_rows[0:P:32, :].rearrange("q (i c) -> q i c", c=32), in_=b_view)
 
         xr_view = xr.rearrange("(a p j) t -> a p j t", p=P, j=PACK)
         raw = [keep.tile([P, PACK, T], F32, name="raw%d" % a) for a in range(PASSES)]
-        for a in range(PASSES):
-            nc.sync.dma_start(out=raw[a][:], in_=xr_view[a])
+        nc.sync.dma_start(out=raw[0][:], in_=xr_view[0])
+        nc.sync.dma_start(out=b_rows[0:P:32, :].rearrange("q (i c) -> q i c", c=32), in_=b_view)
+        nc.sync.dma_start(out=raw[1][:], in_=xr_view[1])
         nc.sync.dma_start(out=wl_words[:].bitcast(I32), in_=ww[:, :, e_words:])
         for r in range(4):
             nc.sync.dma_start(out=wl_scales[:].bitcast(I32)[r:P:32], in_=ws[r, :, :, e_scales:])
@@ -104,13 +105,14 @@ def tile_mix_xres_fm_silu_kernel(tc, x4_words, x4_scales, xr, w4_words, w4_scale
                 in_=grouped[a][:, cols, :].rearrange("p t j -> p (t j)"),
             )
 
-        nc.vector.transpose(b_cols[:, 0:256], b_rows[:, 0:256])
-        nc.vector.transpose(b_cols[:, 256:384], b_rows[:, 256:384])
         for a in range(PASSES):
             for h in range(2):
                 interleave(a, h)
             for h in range(2):
                 quantize(a, h)
+            if a == 0:
+                nc.vector.transpose(b_cols[:, 0:256], b_rows[:, 0:256])
+                nc.vector.transpose(b_cols[:, 256:384], b_rows[:, 256:384])
 
         banks = {}
         done = {}
@@ -152,20 +154,17 @@ def tile_mix_xres_fm_silu_kernel(tc, x4_words, x4_scales, xr, w4_words, w4_scale
 
         def last_tile(i):
             res = keep.tile([P, T], F32, name="res_last")
-            for n in range(4):
-                t0, t1 = n * P, (n + 1) * P
-                acc = psum.tile([P, P], F32, name="acc_last%d" % n, tag="bank%d" % (3 + n))
-                multiply(acc[:], "x4", i, 0, t0, t1, True, False)
-                multiply(acc[:], "x4", i, 1, t0, t1, False, False)
-                multiply(acc[:], "xr", i, 0, t0, t1, False, False)
-                multiply(acc[:], "xr", i, 1, t0, t1, False, True)
+            for n, (t0, t1) in enumerate(LAST):
+                acc = psum.tile([P, t1 - t0], F32, name="acc_last%d" % n, tag="bank%d" % ((i + n) % BANKS))
+                for a in range(PASSES):
+                    multiply(acc[:], "x4", i, a, t0, t1, a == 0, False)
+                for a in range(PASSES):
+                    for t in range(t0, t1, P):
+                        stop = a == PASSES - 1 and t + P == t1
+                        multiply(acc[:, t - t0 : t - t0 + P], "xr", i, a, t, t + P, False, stop)
                 nc.scalar.activation(res[:, t0:t1], acc[:], SILU, bias=b_cols[:, 32 * i : 32 * i + 1])
-                if n == 1:
-                    nc.sync.dma_start(out=out[P * i : P * (i + 1), 0:t1], in_=res[:, 0:t1])
-                if n == 2:
-                    nc.sync.dma_start(out=out[P * i : P * (i + 1), t0:t1], in_=res[:, t0:t1])
-                if n == 3:
-                    nc.scalar.dma_start(out=out[P * i : P * (i + 1), t0:t1], in_=res[:, t0:t1])
+                queue = nc.scalar if t1 == T else nc.sync
+                queue.dma_start(out=out[P * i : P * (i + 1), t0:t1], in_=res[:, t0:t1])
 
         idle = psum.tile([P, T], F32, tag="bank%d" % (BANKS - 1), name="idle")
         for n, width in enumerate(WARM):
@@ -181,15 +180,15 @@ def tile_mix_xres_fm_silu_kernel(tc, x4_words, x4_scales, xr, w4_words, w4_scale
                 stop=n == len(WARM) - 1,
             )
         for a in range(PASSES):
-            for i in range(BANKS):
+            for i in range(EARLY):
                 mx_pass("x4", i, a)
         for i in range(LAG):
             mx_pass("xr", i, 0)
-        for i in range(BANKS):
+        for i in range(EARLY):
             mx_pass("xr", i, 1)
-            if i + LAG < BANKS:
+            if i + LAG < EARLY:
                 mx_pass("xr", i + LAG, 0)
-        for i in range(BANKS, TILES - 1):
+        for i in range(EARLY, TILES - 1):
             for kind in ("x4", "xr"):
                 for a in range(PASSES):
                     mx_pass(kind, i, a)

@@ -19,9 +19,9 @@ PACK = 4
 PASSES = 2
 TILES = M // P
 BANKS = 8
-EARLY = 8
+EARLY = 7
 HALF = T // 2
-LAG = 2
+LAG = 5
 LAST = ((0, 256), (256, 384), (384, 512))
 WARM = (512, 512, 256)
 VECTOR_COLS = 152
@@ -59,7 +59,9 @@ def tile_mix_xres_fm_silu_kernel(tc, x4_words, x4_scales, xr, w4_words, w4_scale
         e_scales = EARLY * P // 4
 
         nc.sync.dma_start(out=x_words[0][:].bitcast(I32), in_=xw[:, 0])
-        nc.gpsimd.dma_start(out=x_words[1][:].bitcast(I32), in_=xw[:, 1])
+        xr_view = xr.rearrange("(a p j) t -> a p j t", p=P, j=PACK)
+        raw = [keep.tile([P, PACK, T], F32, align_bytes=256, name="raw%d" % a) for a in range(PASSES)]
+        nc.gpsimd.dma_start(out=raw[0][:, 0, :], in_=xr_view[0, :, 0, :])
         b_view = b.rearrange("(i q c) -> q i c", q=4, c=32)
 
         for r in range(4):
@@ -71,9 +73,8 @@ def tile_mix_xres_fm_silu_kernel(tc, x4_words, x4_scales, xr, w4_words, w4_scale
             queue.dma_start(out=we_scales[:].bitcast(I32)[r:P:32], in_=ws[r, :, :, 0:e_scales])
         nc.scalar.activation(warm_out[:], warm[:], SILU)
 
-        xr_view = xr.rearrange("(a p j) t -> a p j t", p=P, j=PACK)
-        raw = [keep.tile([P, PACK, T], F32, name="raw%d" % a) for a in range(PASSES)]
-        nc.sync.dma_start(out=raw[0][:], in_=xr_view[0])
+        nc.sync.dma_start(out=raw[0][:, 1:PACK, :], in_=xr_view[0, :, 1:PACK, :])
+        nc.sync.dma_start(out=x_words[1][:].bitcast(I32), in_=xw[:, 1])
         nc.sync.dma_start(out=b_rows[0:P:32, :].rearrange("q (i c) -> q i c", c=32), in_=b_view)
         nc.sync.dma_start(out=raw[1][:], in_=xr_view[1])
         nc.sync.dma_start(out=wl_words[:].bitcast(I32), in_=ww[:, :, e_words:])
@@ -148,12 +149,12 @@ def tile_mix_xres_fm_silu_kernel(tc, x4_words, x4_scales, xr, w4_words, w4_scale
             multiply(banks[i][:], kind, i, a, 0, T, done[i] == 0, done[i] == 3)
             done[i] += 1
             if done[i] == 4:
-                res = keep.tile([P, T], F32, name="res%d" % i)
+                res = keep.tile([P, T], F32, align_bytes=256, name="res%d" % i)
                 nc.scalar.activation(res[:], banks[i][:], SILU, bias=b_cols[:, 32 * i : 32 * i + 1])
                 nc.sync.dma_start(out=out[P * i : P * (i + 1), :], in_=res[:])
 
         def last_tile(i):
-            res = keep.tile([P, T], F32, name="res_last")
+            res = keep.tile([P, T], F32, align_bytes=256, name="res_last")
             for n, (t0, t1) in enumerate(LAST):
                 acc = psum.tile([P, t1 - t0], F32, name="acc_last%d" % n, tag="bank%d" % ((i + n) % BANKS))
                 for a in range(PASSES):

@@ -19,9 +19,9 @@ PACK = 4
 PASSES = 2
 TILES = M // P
 BANKS = 8
-EARLY = 7
+EARLY = BANKS
+BOTH = 4
 HALF = T // 2
-LAG = 5
 LAST = ((0, 256), (256, 384), (384, 512))
 WARM = (512, 512, 256)
 VECTOR_COLS = 152
@@ -36,7 +36,9 @@ def tile_mix_xres_fm_silu_kernel(tc, x4_words, x4_scales, xr, w4_words, w4_scale
 
         x_words = [keep.tile([P, 2 * T], U8, align_bytes=256, name="x_words%d" % a) for a in range(PASSES)]
         x_scales = keep.tile([P, PASSES, T], U8, align_bytes=256)
-        we_words = keep.tile([P, PASSES, EARLY * 2 * P], U8, align_bytes=256)
+        w0_words = keep.tile([P, EARLY * 2 * P], U8, align_bytes=256)
+        w1_words = keep.tile([P, BOTH * 2 * P], U8, align_bytes=256)
+        w2_words = keep.tile([P, (EARLY - BOTH) * 2 * P], U8, align_bytes=256)
         we_scales = keep.tile([P, PASSES, EARLY * P], U8, align_bytes=256)
         wl_words = keep.tile([P, PASSES, (TILES - EARLY) * 2 * P], U8, align_bytes=256)
         wl_scales = keep.tile([P, PASSES, (TILES - EARLY) * P], U8, align_bytes=256)
@@ -55,28 +57,31 @@ def tile_mix_xres_fm_silu_kernel(tc, x4_words, x4_scales, xr, w4_words, w4_scale
         ww = w4_words.bitcast(I32).rearrange("a p n -> p a n")
         xs = x4_scales.bitcast(I32).rearrange("a (q r) n -> r q a n", r=4)
         ws = w4_scales.bitcast(I32).rearrange("a (q r) n -> r q a n", r=4)
+        b_words = BOTH * 2 * P // 4
         e_words = EARLY * 2 * P // 4
         e_scales = EARLY * P // 4
 
         nc.sync.dma_start(out=x_words[0][:].bitcast(I32), in_=xw[:, 0])
         xr_view = xr.rearrange("(a p j) t -> a p j t", p=P, j=PACK)
         raw = [keep.tile([P, PACK, T], F32, align_bytes=256, name="raw%d" % a) for a in range(PASSES)]
-        nc.gpsimd.dma_start(out=raw[0][:, 0, :], in_=xr_view[0, :, 0, :])
+        nc.gpsimd.dma_start(out=raw[0][:, 0:2, :], in_=xr_view[0, :, 0:2, :])
         b_view = b.rearrange("(i q c) -> q i c", q=4, c=32)
 
         for r in range(4):
             queue = nc.scalar if r < 2 else nc.sync
             queue.dma_start(out=x_scales[:].bitcast(I32)[r:P:32], in_=xs[r])
-        nc.scalar.dma_start(out=we_words[:].bitcast(I32), in_=ww[:, :, 0:e_words])
+        nc.scalar.dma_start(out=w0_words[:].bitcast(I32), in_=ww[:, 0, 0:e_words])
         for r in range(4):
             queue = nc.scalar if r == 1 else nc.sync
             queue.dma_start(out=we_scales[:].bitcast(I32)[r:P:32], in_=ws[r, :, :, 0:e_scales])
         nc.scalar.activation(warm_out[:], warm[:], SILU)
 
-        nc.sync.dma_start(out=raw[0][:, 1:PACK, :], in_=xr_view[0, :, 1:PACK, :])
+        nc.sync.dma_start(out=raw[0][:, 2:PACK, :], in_=xr_view[0, :, 2:PACK, :])
         nc.sync.dma_start(out=x_words[1][:].bitcast(I32), in_=xw[:, 1])
+        nc.sync.dma_start(out=w1_words[:].bitcast(I32), in_=ww[:, 1, 0:b_words])
         nc.sync.dma_start(out=b_rows[0:P:32, :].rearrange("q (i c) -> q i c", c=32), in_=b_view)
         nc.sync.dma_start(out=raw[1][:], in_=xr_view[1])
+        nc.sync.dma_start(out=w2_words[:].bitcast(I32), in_=ww[:, 1, b_words:e_words])
         nc.sync.dma_start(out=wl_words[:].bitcast(I32), in_=ww[:, :, e_words:])
         for r in range(4):
             nc.sync.dma_start(out=wl_scales[:].bitcast(I32)[r:P:32], in_=ws[r, :, :, e_scales:])
@@ -120,8 +125,9 @@ def tile_mix_xres_fm_silu_kernel(tc, x4_words, x4_scales, xr, w4_words, w4_scale
 
         def stationary(i, a):
             if i < EARLY:
+                words, k = (w0_words, i) if a == 0 else (w1_words, i) if i < BOTH else (w2_words, i - BOTH)
                 return (
-                    we_words[:, a, 2 * P * i : 2 * P * (i + 1)].bitcast(FP4X4),
+                    words[:, 2 * P * k : 2 * P * (k + 1)].bitcast(FP4X4),
                     we_scales[:, a, P * i : P * (i + 1)],
                 )
             k = i - EARLY
@@ -180,15 +186,16 @@ def tile_mix_xres_fm_silu_kernel(tc, x4_words, x4_scales, xr, w4_words, w4_scale
                 start=n == 0,
                 stop=n == len(WARM) - 1,
             )
-        for a in range(PASSES):
-            for i in range(EARLY):
-                mx_pass("x4", i, a)
-        for i in range(LAG):
+        for i in range(EARLY):
+            mx_pass("x4", i, 0)
+        for i in range(BOTH):
+            mx_pass("x4", i, 1)
+        for i in range(EARLY):
             mx_pass("xr", i, 0)
         for i in range(EARLY):
+            if i >= BOTH:
+                mx_pass("x4", i, 1)
             mx_pass("xr", i, 1)
-            if i + LAG < EARLY:
-                mx_pass("xr", i + LAG, 0)
         for i in range(EARLY, TILES - 1):
             for kind in ("x4", "xr"):
                 for a in range(PASSES):

@@ -79,9 +79,9 @@ def tile_mix_xres_fm_silu_kernel(tc, x4_words, x4_scales, xr, w4_words, w4_scale
         nc.sync.dma_start(out=raw[0][:, 2:PACK, :], in_=xr_view[0, :, 2:PACK, :])
         nc.sync.dma_start(out=x_words[1][:].bitcast(I32), in_=xw[:, 1])
         nc.sync.dma_start(out=w1_words[:].bitcast(I32), in_=ww[:, 1, 0:b_words])
-        nc.sync.dma_start(out=b_rows[0:P:32, :].rearrange("q (i c) -> q i c", c=32), in_=b_view)
         nc.sync.dma_start(out=raw[1][:], in_=xr_view[1])
         nc.sync.dma_start(out=w2_words[:].bitcast(I32), in_=ww[:, 1, b_words:e_words])
+        nc.sync.dma_start(out=b_rows[0:P:32, :].rearrange("q (i c) -> q i c", c=32), in_=b_view)
         nc.sync.dma_start(out=wl_words[:].bitcast(I32), in_=ww[:, :, e_words:])
         for r in range(4):
             nc.sync.dma_start(out=wl_scales[:].bitcast(I32)[r:P:32], in_=ws[r, :, :, e_scales:])
@@ -116,9 +116,8 @@ def tile_mix_xres_fm_silu_kernel(tc, x4_words, x4_scales, xr, w4_words, w4_scale
                 interleave(a, h)
             for h in range(2):
                 quantize(a, h)
-            if a == 0:
-                nc.vector.transpose(b_cols[:, 0:256], b_rows[:, 0:256])
-                nc.vector.transpose(b_cols[:, 256:384], b_rows[:, 256:384])
+        nc.vector.transpose(b_cols[:, 0:128], b_rows[:, 0:128])
+        nc.vector.transpose(b_cols[:, 128:384], b_rows[:, 128:384])
 
         banks = {}
         done = {}
@@ -156,8 +155,11 @@ def tile_mix_xres_fm_silu_kernel(tc, x4_words, x4_scales, xr, w4_words, w4_scale
             done[i] += 1
             if done[i] == 4:
                 res = keep.tile([P, T], F32, align_bytes=256, name="res%d" % i)
-                nc.scalar.activation(res[:], banks[i][:], SILU, bias=b_cols[:, 32 * i : 32 * i + 1])
-                nc.sync.dma_start(out=out[P * i : P * (i + 1), :], in_=res[:])
+                width = HALF if i in (0, TILES - 2) else T
+                for t in range(0, T, width):
+                    cols = slice(t, t + width)
+                    nc.scalar.activation(res[:, cols], banks[i][:, cols], SILU, bias=b_cols[:, 32 * i : 32 * i + 1])
+                    nc.sync.dma_start(out=out[P * i : P * (i + 1), cols], in_=res[:, cols])
 
         def last_tile(i):
             res = keep.tile([P, T], F32, align_bytes=256, name="res_last")

@@ -23,7 +23,7 @@ EARLY = BANKS
 BOTH = 4
 HALF = T // 2
 LAST = ((0, 256), (256, 384), (384, 512))
-WARM = (512, 512, 256)
+WARM = (512, 512, 512)
 VECTOR_COLS = 152
 
 

@@ -20,11 +20,11 @@ PASSES = 2
 TILES = M // P
 BANKS = 8
 EARLY = BANKS
-BOTH = 4
-HALF = T // 2
+XR_LOADS = (((0, 128), (128, 256), (256, 512)), ((0, 256), (256, 512)))
+XR_STEPS = (((0, 128), (128, 256), (256, 384), (384, 512)), ((0, 256), (256, 512)))
+VECTOR_COLS = {128: 64, 256: 144}
 LAST = ((0, 256), (256, 384), (384, 512))
-WARM = (512, 512, 512)
-VECTOR_COLS = 152
+HALF = T // 2
 
 
 def tile_mix_xres_fm_silu_kernel(tc, x4_words, x4_scales, xr, w4_words, w4_scales, b, out):
@@ -34,22 +34,23 @@ def tile_mix_xres_fm_silu_kernel(tc, x4_words, x4_scales, xr, w4_words, w4_scale
         psum = ctx.enter_context(tc.psum_pool(name="psum", bufs=1))
         ctx.enter_context(tc.manual_schedule())
 
-        x_words = [keep.tile([P, 2 * T], U8, align_bytes=256, name="x_words%d" % a) for a in range(PASSES)]
-        x_scales = keep.tile([P, PASSES, T], U8, align_bytes=256)
-        w0_words = keep.tile([P, EARLY * 2 * P], U8, align_bytes=256)
-        w1_words = keep.tile([P, BOTH * 2 * P], U8, align_bytes=256)
-        w2_words = keep.tile([P, (EARLY - BOTH) * 2 * P], U8, align_bytes=256)
-        we_scales = keep.tile([P, PASSES, EARLY * P], U8, align_bytes=256)
-        wl_words = keep.tile([P, PASSES, (TILES - EARLY) * 2 * P], U8, align_bytes=256)
-        wl_scales = keep.tile([P, PASSES, (TILES - EARLY) * P], U8, align_bytes=256)
+        def byte_tile(name, *shape):
+            return keep.tile([P, *shape], U8, align_bytes=256, name=name)
+
+        x_words = [byte_tile("x_words%d" % a, 2 * T) for a in range(PASSES)]
+        x_scales = byte_tile("x_scales", PASSES, T)
+        we_words = [byte_tile("we_words%d" % a, EARLY * 2 * P) for a in range(PASSES)]
+        we_scales = byte_tile("we_scales", PASSES, EARLY * P)
+        wl_words = byte_tile("wl_words", PASSES, (TILES - EARLY) * 2 * P)
+        wl_scales = byte_tile("wl_scales", PASSES, (TILES - EARLY) * P)
         warm = keep.tile([P, 1], F32)
         warm_out = keep.tile([P, 1], F32)
         b_rows = keep.tile([P, TILES * 32], F32, align_bytes=64)
         b_cols = keep.tile([P, TILES * 32], F32, align_bytes=64)
 
-        nc.vector.memset(x_scales[:].bitcast(I32), 0)
         nc.vector.memset(we_scales[:].bitcast(I32), 0)
         nc.vector.memset(warm[:], 0.0)
+        nc.vector.memset(x_scales[:].bitcast(I32), 0)
         nc.vector.memset(b_rows[:], 0.0)
         nc.vector.memset(wl_scales[:].bitcast(I32), 0)
 
@@ -57,30 +58,36 @@ def tile_mix_xres_fm_silu_kernel(tc, x4_words, x4_scales, xr, w4_words, w4_scale
         ww = w4_words.bitcast(I32).rearrange("a p n -> p a n")
         xs = x4_scales.bitcast(I32).rearrange("a (q r) n -> r q a n", r=4)
         ws = w4_scales.bitcast(I32).rearrange("a (q r) n -> r q a n", r=4)
-        b_words = BOTH * 2 * P // 4
+        xr_view = xr.rearrange("(a p j) t -> a p j t", p=P, j=PACK)
+        b_view = b.rearrange("(i q c) -> q i c", q=4, c=32)
         e_words = EARLY * 2 * P // 4
         e_scales = EARLY * P // 4
 
-        nc.sync.dma_start(out=x_words[0][:].bitcast(I32), in_=xw[:, 0])
-        xr_view = xr.rearrange("(a p j) t -> a p j t", p=P, j=PACK)
-        raw = [keep.tile([P, PACK, T], F32, align_bytes=256, name="raw%d" % a) for a in range(PASSES)]
-        nc.gpsimd.dma_start(out=raw[0][:, 0:2, :], in_=xr_view[0, :, 0:2, :])
-        b_view = b.rearrange("(i q c) -> q i c", q=4, c=32)
+        raw = {}
 
-        for r in range(4):
-            queue = nc.scalar if r < 2 else nc.sync
-            queue.dma_start(out=x_scales[:].bitcast(I32)[r:P:32], in_=xs[r])
-        nc.scalar.dma_start(out=w0_words[:].bitcast(I32), in_=ww[:, 0, 0:e_words])
-        for r in range(4):
-            queue = nc.scalar if r == 1 else nc.sync
-            queue.dma_start(out=we_scales[:].bitcast(I32)[r:P:32], in_=ws[r, :, :, 0:e_scales])
+        def load_xr(queue, a, n):
+            t0, t1 = XR_LOADS[a][n]
+            piece = keep.tile([P, PACK, t1 - t0], F32, align_bytes=256, name="raw%d_%d" % (a, n))
+            queue.dma_start(out=piece[:], in_=xr_view[a, :, :, t0:t1])
+            for s0, s1 in XR_STEPS[a]:
+                if t0 <= s0 < t1:
+                    raw[a, s0] = piece[:, :, s0 - t0 : s1 - t0]
+
+        load_xr(nc.scalar, 0, 0)
+        nc.scalar.dma_start(out=we_words[0][:].bitcast(I32), in_=ww[:, 0, 0:e_words])
+        load_xr(nc.scalar, 0, 1)
         nc.scalar.activation(warm_out[:], warm[:], SILU)
+        for r in range(4):
+            nc.sync.dma_start(out=we_scales[:].bitcast(I32)[r:P:32], in_=ws[r, :, :, 0:e_scales])
+        load_xr(nc.sync, 0, 2)
 
-        nc.sync.dma_start(out=raw[0][:, 2:PACK, :], in_=xr_view[0, :, 2:PACK, :])
+        load_xr(nc.sync, 1, 0)
+        for r in range(4):
+            nc.sync.dma_start(out=x_scales[:].bitcast(I32)[r:P:32], in_=xs[r])
+        nc.sync.dma_start(out=x_words[0][:].bitcast(I32), in_=xw[:, 0])
+        load_xr(nc.sync, 1, 1)
         nc.sync.dma_start(out=x_words[1][:].bitcast(I32), in_=xw[:, 1])
-        nc.sync.dma_start(out=w1_words[:].bitcast(I32), in_=ww[:, 1, 0:b_words])
-        nc.sync.dma_start(out=raw[1][:], in_=xr_view[1])
-        nc.sync.dma_start(out=w2_words[:].bitcast(I32), in_=ww[:, 1, b_words:e_words])
+        nc.sync.dma_start(out=we_words[1][:].bitcast(I32), in_=ww[:, 1, 0:e_words])
         nc.sync.dma_start(out=b_rows[0:P:32, :].rearrange("q (i c) -> q i c", c=32), in_=b_view)
         nc.sync.dma_start(out=wl_words[:].bitcast(I32), in_=ww[:, :, e_words:])
         for r in range(4):
@@ -90,43 +97,29 @@ def tile_mix_xres_fm_silu_kernel(tc, x4_words, x4_scales, xr, w4_words, w4_scale
         codes = [keep.tile([P, T], U32, align_bytes=256, name="codes%d" % a) for a in range(PASSES)]
         scales = [keep.tile([P, T], U8, align_bytes=256, name="scales%d" % a) for a in range(PASSES)]
 
-        def interleave(a, h):
-            c0 = h * HALF
-            c1 = c0 + VECTOR_COLS
-            c2 = c0 + HALF
-            nc.vector.tensor_copy(
-                out=grouped[a][:, c0:c1, :].rearrange("p (c i) j -> p c j i", i=4),
-                in_=raw[a][:, :, c0:c1].rearrange("p j (c i) -> p c j i", i=4),
-            )
-            nc.scalar.copy(
-                out=grouped[a][:, c1:c2, :].rearrange("p (c i) j -> p c j i", i=4),
-                in_=raw[a][:, :, c1:c2].rearrange("p j (c i) -> p c j i", i=4),
-            )
-
-        def quantize(a, h):
-            cols = slice(h * HALF, (h + 1) * HALF)
-            nc.vector.quantize_mx(
-                out=codes[a][:, cols].bitcast(FP8X4),
-                scales=scales[a][:, cols],
-                in_=grouped[a][:, cols, :].rearrange("p t j -> p (t j)"),
-            )
-
         for a in range(PASSES):
-            for h in range(2):
-                interleave(a, h)
-            for h in range(2):
-                quantize(a, h)
+            for t0, t1 in XR_STEPS[a]:
+                split = VECTOR_COLS[t1 - t0]
+                nc.vector.tensor_copy(
+                    out=grouped[a][:, t0 : t0 + split, :].rearrange("p (c i) j -> p c j i", i=4),
+                    in_=raw[a, t0][:, :, 0:split].rearrange("p j (c i) -> p c j i", i=4),
+                )
+                nc.scalar.copy(
+                    out=grouped[a][:, t0 + split : t1, :].rearrange("p (c i) j -> p c j i", i=4),
+                    in_=raw[a, t0][:, :, split:].rearrange("p j (c i) -> p c j i", i=4),
+                )
+                nc.vector.quantize_mx(
+                    out=codes[a][:, t0:t1].bitcast(FP8X4),
+                    scales=scales[a][:, t0:t1],
+                    in_=grouped[a][:, t0:t1, :].rearrange("p t j -> p (t j)"),
+                )
         nc.vector.transpose(b_cols[:, 0:128], b_rows[:, 0:128])
         nc.vector.transpose(b_cols[:, 128:384], b_rows[:, 128:384])
 
-        banks = {}
-        done = {}
-
         def stationary(i, a):
             if i < EARLY:
-                words, k = (w0_words, i) if a == 0 else (w1_words, i) if i < BOTH else (w2_words, i - BOTH)
                 return (
-                    words[:, 2 * P * k : 2 * P * (k + 1)].bitcast(FP4X4),
+                    we_words[a][:, 2 * P * i : 2 * P * (i + 1)].bitcast(FP4X4),
                     we_scales[:, a, P * i : P * (i + 1)],
                 )
             k = i - EARLY
@@ -135,71 +128,54 @@ def tile_mix_xres_fm_silu_kernel(tc, x4_words, x4_scales, xr, w4_words, w4_scale
                 wl_scales[:, a, P * k : P * (k + 1)],
             )
 
-        def moving(kind, a, t0, t1):
-            if kind == "x4":
-                return x_words[a][:, 2 * t0 : 2 * t1].bitcast(FP4X4), x_scales[:, a, t0:t1]
-            return codes[a][:, t0:t1].bitcast(FP8X4), scales[a][:, t0:t1]
-
-        def multiply(acc, kind, i, a, t0, t1, start, stop):
+        def multiply(acc, kind, i, a, t0, t1, start=False, stop=False):
             w_view, w_scale = stationary(i, a)
-            x_view, x_scale = moving(kind, a, t0, t1)
+            if kind == "x4":
+                x_view, x_scale = x_words[a][:, 2 * t0 : 2 * t1].bitcast(FP4X4), x_scales[:, a, t0:t1]
+            else:
+                x_view, x_scale = codes[a][:, t0:t1].bitcast(FP8X4), scales[a][:, t0:t1]
             nc.tensor.matmul_mx(
                 out=acc, lhsT=w_view, lhsT_scale=w_scale, rhs=x_view, rhs_scale=x_scale, start=start, stop=stop
             )
 
-        def mx_pass(kind, i, a):
-            if i not in banks:
-                banks[i] = psum.tile([P, T], F32, name="acc%d" % i, tag="bank%d" % (i % BANKS))
-                done[i] = 0
-            multiply(banks[i][:], kind, i, a, 0, T, done[i] == 0, done[i] == 3)
-            done[i] += 1
-            if done[i] == 4:
-                res = keep.tile([P, T], F32, align_bytes=256, name="res%d" % i)
-                width = HALF if i in (0, TILES - 2) else T
-                for t in range(0, T, width):
-                    cols = slice(t, t + width)
-                    nc.scalar.activation(res[:, cols], banks[i][:, cols], SILU, bias=b_cols[:, 32 * i : 32 * i + 1])
-                    nc.sync.dma_start(out=out[P * i : P * (i + 1), cols], in_=res[:, cols])
+        def open_bank(i):
+            return psum.tile([P, T], F32, name="acc%d" % i, tag="bank%d" % (i % BANKS))
 
-        def last_tile(i):
-            res = keep.tile([P, T], F32, align_bytes=256, name="res_last")
-            for n, (t0, t1) in enumerate(LAST):
-                acc = psum.tile([P, t1 - t0], F32, name="acc_last%d" % n, tag="bank%d" % ((i + n) % BANKS))
-                for a in range(PASSES):
-                    multiply(acc[:], "x4", i, a, t0, t1, a == 0, False)
-                for a in range(PASSES):
-                    for t in range(t0, t1, P):
-                        stop = a == PASSES - 1 and t + P == t1
-                        multiply(acc[:, t - t0 : t - t0 + P], "xr", i, a, t, t + P, False, stop)
-                nc.scalar.activation(res[:, t0:t1], acc[:], SILU, bias=b_cols[:, 32 * i : 32 * i + 1])
-                queue = nc.scalar if t1 == T else nc.sync
-                queue.dma_start(out=out[P * i : P * (i + 1), t0:t1], in_=res[:, t0:t1])
+        def finish(i, acc):
+            res = keep.tile([P, T], F32, align_bytes=256, name="res%d" % i)
+            width = HALF if i in (0, TILES - 2) else T
+            for t in range(0, T, width):
+                cols = slice(t, t + width)
+                nc.scalar.activation(res[:, cols], acc[:, cols], SILU, bias=b_cols[:, 32 * i : 32 * i + 1])
+                nc.sync.dma_start(out=out[P * i : P * (i + 1), cols], in_=res[:, cols])
 
-        idle = psum.tile([P, T], F32, tag="bank%d" % (BANKS - 1), name="idle")
-        for n, width in enumerate(WARM):
-            x_view, x_scale = moving("x4", 0, 0, width)
-            s_view, s_scale = moving("x4", 0, 0, P)
-            nc.tensor.matmul_mx(
-                out=idle[:, 0:width],
-                lhsT=s_view,
-                lhsT_scale=s_scale,
-                rhs=x_view,
-                rhs_scale=x_scale,
-                start=n == 0,
-                stop=n == len(WARM) - 1,
-            )
+        banks = [open_bank(i) for i in range(EARLY)]
+        for t0, t1 in XR_STEPS[0]:
+            for i in range(EARLY):
+                multiply(banks[i][:, t0:t1], "xr", i, 0, t0, t1, start=t0 == 0)
         for i in range(EARLY):
-            mx_pass("x4", i, 0)
-        for i in range(BOTH):
-            mx_pass("x4", i, 1)
+            multiply(banks[i][:], "x4", i, 0, 0, T)
         for i in range(EARLY):
-            mx_pass("xr", i, 0)
-        for i in range(EARLY):
-            if i >= BOTH:
-                mx_pass("x4", i, 1)
-            mx_pass("xr", i, 1)
+            multiply(banks[i][:], "x4", i, 1, 0, T)
+            multiply(banks[i][:], "xr", i, 1, 0, T, stop=True)
+            finish(i, banks[i])
         for i in range(EARLY, TILES - 1):
+            acc = open_bank(i)
             for kind in ("x4", "xr"):
                 for a in range(PASSES):
-                    mx_pass(kind, i, a)
-        last_tile(TILES - 1)
+                    multiply(acc[:], kind, i, a, 0, T, start=(kind, a) == ("x4", 0), stop=(kind, a) == ("xr", 1))
+            finish(i, acc)
+
+        i = TILES - 1
+        res = keep.tile([P, T], F32, align_bytes=256, name="res_last")
+        for n, (t0, t1) in enumerate(LAST):
+            acc = psum.tile([P, t1 - t0], F32, name="acc_last%d" % n, tag="bank%d" % ((i + n) % BANKS))
+            for a in range(PASSES):
+                multiply(acc[:], "x4", i, a, t0, t1, start=a == 0)
+            for a in range(PASSES):
+                for t in range(t0, t1, P):
+                    stop = a == PASSES - 1 and t + P == t1
+                    multiply(acc[:, t - t0 : t - t0 + P], "xr", i, a, t, t + P, stop=stop)
+            nc.scalar.activation(res[:, t0:t1], acc[:], SILU, bias=b_cols[:, 32 * i : 32 * i + 1])
+            queue = nc.scalar if t1 == T else nc.sync
+            queue.dma_start(out=out[P * i : P * (i + 1), t0:t1], in_=res[:, t0:t1])

@@ -20,7 +20,7 @@ PASSES = 2
 TILES = M // P
 BANKS = 8
 EARLY = BANKS
-XR_LOADS = (((0, 128), (128, 256), (256, 512)), ((0, 256), (256, 512)))
+BOTH = 3
 XR_STEPS = (((0, 128), (128, 256), (256, 384), (384, 512)), ((0, 256), (256, 512)))
 VECTOR_COLS = {128: 64, 256: 144}
 LAST = ((0, 256), (256, 384), (384, 512))
@@ -37,9 +37,11 @@ def tile_mix_xres_fm_silu_kernel(tc, x4_words, x4_scales, xr, w4_words, w4_scale
         def byte_tile(name, *shape):
             return keep.tile([P, *shape], U8, align_bytes=256, name=name)
 
-        x_words = [byte_tile("x_words%d" % a, 2 * T) for a in range(PASSES)]
+        x_words = byte_tile("x_words", PASSES, 2 * T)
         x_scales = byte_tile("x_scales", PASSES, T)
-        we_words = [byte_tile("we_words%d" % a, EARLY * 2 * P) for a in range(PASSES)]
+        w0_words = byte_tile("w0_words", EARLY * 2 * P)
+        w1_words = byte_tile("w1_words", BOTH * 2 * P)
+        w2_words = byte_tile("w2_words", (EARLY - BOTH) * 2 * P)
         we_scales = byte_tile("we_scales", PASSES, EARLY * P)
         wl_words = byte_tile("wl_words", PASSES, (TILES - EARLY) * 2 * P)
         wl_scales = byte_tile("wl_scales", PASSES, (TILES - EARLY) * P)
@@ -60,34 +62,31 @@ def tile_mix_xres_fm_silu_kernel(tc, x4_words, x4_scales, xr, w4_words, w4_scale
         ws = w4_scales.bitcast(I32).rearrange("a (q r) n -> r q a n", r=4)
         xr_view = xr.rearrange("(a p j) t -> a p j t", p=P, j=PACK)
         b_view = b.rearrange("(i q c) -> q i c", q=4, c=32)
+        b_words = BOTH * 2 * P // 4
         e_words = EARLY * 2 * P // 4
         e_scales = EARLY * P // 4
 
         raw = {}
 
         def load_xr(queue, a, n):
-            t0, t1 = XR_LOADS[a][n]
-            piece = keep.tile([P, PACK, t1 - t0], F32, align_bytes=256, name="raw%d_%d" % (a, n))
-            queue.dma_start(out=piece[:], in_=xr_view[a, :, :, t0:t1])
-            for s0, s1 in XR_STEPS[a]:
-                if t0 <= s0 < t1:
-                    raw[a, s0] = piece[:, :, s0 - t0 : s1 - t0]
+            t0, t1 = XR_STEPS[a][n]
+            raw[a, t0] = keep.tile([P, PACK, t1 - t0], F32, align_bytes=256, name="raw%d_%d" % (a, n))
+            queue.dma_start(out=raw[a, t0][:], in_=xr_view[a, :, :, t0:t1])
 
         load_xr(nc.scalar, 0, 0)
-        nc.scalar.dma_start(out=we_words[0][:].bitcast(I32), in_=ww[:, 0, 0:e_words])
-        load_xr(nc.scalar, 0, 1)
+        nc.scalar.dma_start(out=w0_words[:].bitcast(I32), in_=ww[:, 0, 0:e_words])
         nc.scalar.activation(warm_out[:], warm[:], SILU)
         for r in range(4):
             nc.sync.dma_start(out=we_scales[:].bitcast(I32)[r:P:32], in_=ws[r, :, :, 0:e_scales])
-        load_xr(nc.sync, 0, 2)
-
-        load_xr(nc.sync, 1, 0)
+        for n in range(1, 4):
+            load_xr(nc.sync, 0, n)
         for r in range(4):
             nc.sync.dma_start(out=x_scales[:].bitcast(I32)[r:P:32], in_=xs[r])
-        nc.sync.dma_start(out=x_words[0][:].bitcast(I32), in_=xw[:, 0])
+        nc.sync.dma_start(out=x_words[:].bitcast(I32), in_=xw)
+        load_xr(nc.sync, 1, 0)
+        nc.sync.dma_start(out=w1_words[:].bitcast(I32), in_=ww[:, 1, 0:b_words])
         load_xr(nc.sync, 1, 1)
-        nc.sync.dma_start(out=x_words[1][:].bitcast(I32), in_=xw[:, 1])
-        nc.sync.dma_start(out=we_words[1][:].bitcast(I32), in_=ww[:, 1, 0:e_words])
+        nc.sync.dma_start(out=w2_words[:].bitcast(I32), in_=ww[:, 1, b_words:e_words])
         nc.sync.dma_start(out=b_rows[0:P:32, :].rearrange("q (i c) -> q i c", c=32), in_=b_view)
         nc.sync.dma_start(out=wl_words[:].bitcast(I32), in_=ww[:, :, e_words:])
         for r in range(4):
@@ -118,8 +117,9 @@ def tile_mix_xres_fm_silu_kernel(tc, x4_words, x4_scales, xr, w4_words, w4_scale
 
         def stationary(i, a):
             if i < EARLY:
+                words, k = (w0_words, i) if a == 0 else (w1_words, i) if i < BOTH else (w2_words, i - BOTH)
                 return (
-                    we_words[a][:, 2 * P * i : 2 * P * (i + 1)].bitcast(FP4X4),
+                    words[:, 2 * P * k : 2 * P * (k + 1)].bitcast(FP4X4),
                     we_scales[:, a, P * i : P * (i + 1)],
                 )
             k = i - EARLY
@@ -131,7 +131,7 @@ def tile_mix_xres_fm_silu_kernel(tc, x4_words, x4_scales, xr, w4_words, w4_scale
         def multiply(acc, kind, i, a, t0, t1, start=False, stop=False):
             w_view, w_scale = stationary(i, a)
             if kind == "x4":
-                x_view, x_scale = x_words[a][:, 2 * t0 : 2 * t1].bitcast(FP4X4), x_scales[:, a, t0:t1]
+                x_view, x_scale = x_words[:, a, 2 * t0 : 2 * t1].bitcast(FP4X4), x_scales[:, a, t0:t1]
             else:
                 x_view, x_scale = codes[a][:, t0:t1].bitcast(FP8X4), scales[a][:, t0:t1]
             nc.tensor.matmul_mx(
@@ -155,8 +155,11 @@ def tile_mix_xres_fm_silu_kernel(tc, x4_words, x4_scales, xr, w4_words, w4_scale
                 multiply(banks[i][:, t0:t1], "xr", i, 0, t0, t1, start=t0 == 0)
         for i in range(EARLY):
             multiply(banks[i][:], "x4", i, 0, 0, T)
-        for i in range(EARLY):
+        for i in range(BOTH):
             multiply(banks[i][:], "x4", i, 1, 0, T)
+        for i in range(EARLY):
+            if i >= BOTH:
+                multiply(banks[i][:], "x4", i, 1, 0, T)
             multiply(banks[i][:], "xr", i, 1, 0, T, stop=True)
             finish(i, banks[i])
         for i in range(EARLY, TILES - 1):

@@ -21,8 +21,9 @@ TILES = M // P
 BANKS = 8
 EARLY = BANKS
 BOTH = 3
+FIRST = 4
 XR_STEPS = (((0, 128), (128, 256), (256, 384), (384, 512)), ((0, 256), (256, 512)))
-VECTOR_COLS = {128: 64, 256: 144}
+VECTOR_COLS = {128: 56, 256: 144}
 LAST = ((0, 256), (256, 384), (384, 512))
 HALF = T // 2
 
@@ -39,7 +40,8 @@ def tile_mix_xres_fm_silu_kernel(tc, x4_words, x4_scales, xr, w4_words, w4_scale
 
         x_words = byte_tile("x_words", PASSES, 2 * T)
         x_scales = byte_tile("x_scales", PASSES, T)
-        w0_words = byte_tile("w0_words", EARLY * 2 * P)
+        wa_words = byte_tile("wa_words", FIRST * 2 * P)
+        wb_words = byte_tile("wb_words", (EARLY - FIRST) * 2 * P)
         w1_words = byte_tile("w1_words", BOTH * 2 * P)
         w2_words = byte_tile("w2_words", (EARLY - BOTH) * 2 * P)
         we_scales = byte_tile("we_scales", PASSES, EARLY * P)
@@ -63,6 +65,7 @@ def tile_mix_xres_fm_silu_kernel(tc, x4_words, x4_scales, xr, w4_words, w4_scale
         xr_view = xr.rearrange("(a p j) t -> a p j t", p=P, j=PACK)
         b_view = b.rearrange("(i q c) -> q i c", q=4, c=32)
         b_words = BOTH * 2 * P // 4
+        f_words = FIRST * 2 * P // 4
         e_words = EARLY * 2 * P // 4
         e_scales = EARLY * P // 4
 
@@ -74,12 +77,14 @@ def tile_mix_xres_fm_silu_kernel(tc, x4_words, x4_scales, xr, w4_words, w4_scale
             queue.dma_start(out=raw[a, t0][:], in_=xr_view[a, :, :, t0:t1])
 
         load_xr(nc.scalar, 0, 0)
-        nc.scalar.dma_start(out=w0_words[:].bitcast(I32), in_=ww[:, 0, 0:e_words])
+        nc.scalar.dma_start(out=wa_words[:].bitcast(I32), in_=ww[:, 0, 0:f_words])
         nc.scalar.activation(warm_out[:], warm[:], SILU)
         for r in range(4):
             nc.sync.dma_start(out=we_scales[:].bitcast(I32)[r:P:32], in_=ws[r, :, :, 0:e_scales])
-        for n in range(1, 4):
-            load_xr(nc.sync, 0, n)
+        load_xr(nc.sync, 0, 1)
+        nc.sync.dma_start(out=wb_words[:].bitcast(I32), in_=ww[:, 0, f_words:e_words])
+        load_xr(nc.sync, 0, 2)
+        load_xr(nc.sync, 0, 3)
         for r in range(4):
             nc.sync.dma_start(out=x_scales[:].bitcast(I32)[r:P:32], in_=xs[r])
         nc.sync.dma_start(out=x_words[:].bitcast(I32), in_=xw)
@@ -117,7 +122,8 @@ def tile_mix_xres_fm_silu_kernel(tc, x4_words, x4_scales, xr, w4_words, w4_scale
 
         def stationary(i, a):
             if i < EARLY:
-                words, k = (w0_words, i) if a == 0 else (w1_words, i) if i < BOTH else (w2_words, i - BOTH)
+                cut, below, above = (FIRST, wa_words, wb_words) if a == 0 else (BOTH, w1_words, w2_words)
+                words, k = (below, i) if i < cut else (above, i - cut)
                 return (
                     words[:, 2 * P * k : 2 * P * (k + 1)].bitcast(FP4X4),
                     we_scales[:, a, P * i : P * (i + 1)],

@@ -60,8 +60,8 @@ def tile_mix_xres_fm_silu_kernel(tc, x4_words, x4_scales, xr, w4_words, w4_scale
 
         xw = x4_words.bitcast(I32).rearrange("a p n -> p a n")
         ww = w4_words.bitcast(I32).rearrange("a p n -> p a n")
-        xs = x4_scales.bitcast(I32).rearrange("a (q r) n -> r q a n", r=4)
-        ws = w4_scales.bitcast(I32).rearrange("a (q r) n -> r q a n", r=4)
+        xs = x4_scales.bitcast(I32).rearrange("a (q r) n -> q r a n", r=4)
+        ws = w4_scales.bitcast(I32).rearrange("a (q r) n -> q r a n", r=4)
         xr_view = xr.rearrange("(a p j) t -> a p j t", p=P, j=PACK)
         b_view = b.rearrange("(i q c) -> q i c", q=4, c=32)
         b_words = BOTH * 2 * P // 4
@@ -79,14 +79,14 @@ def tile_mix_xres_fm_silu_kernel(tc, x4_words, x4_scales, xr, w4_words, w4_scale
         load_xr(nc.scalar, 0, 0)
         nc.scalar.dma_start(out=wa_words[:].bitcast(I32), in_=ww[:, 0, 0:f_words])
         nc.scalar.activation(warm_out[:], warm[:], SILU)
-        for r in range(4):
-            nc.sync.dma_start(out=we_scales[:].bitcast(I32)[r:P:32], in_=ws[r, :, :, 0:e_scales])
+        for q in range(4):
+            nc.sync.dma_start(out=we_scales[:].bitcast(I32)[32 * q : 32 * q + 4], in_=ws[q, :, :, 0:e_scales])
         load_xr(nc.sync, 0, 1)
         nc.sync.dma_start(out=wb_words[:].bitcast(I32), in_=ww[:, 0, f_words:e_words])
         load_xr(nc.sync, 0, 2)
         load_xr(nc.sync, 0, 3)
-        for r in range(4):
-            nc.sync.dma_start(out=x_scales[:].bitcast(I32)[r:P:32], in_=xs[r])
+        for q in range(4):
+            nc.sync.dma_start(out=x_scales[:].bitcast(I32)[32 * q : 32 * q + 4], in_=xs[q])
         nc.sync.dma_start(out=x_words[:].bitcast(I32), in_=xw)
         load_xr(nc.sync, 1, 0)
         nc.sync.dma_start(out=w1_words[:].bitcast(I32), in_=ww[:, 1, 0:b_words])
@@ -94,8 +94,8 @@ def tile_mix_xres_fm_silu_kernel(tc, x4_words, x4_scales, xr, w4_words, w4_scale
         nc.sync.dma_start(out=w2_words[:].bitcast(I32), in_=ww[:, 1, b_words:e_words])
         nc.sync.dma_start(out=b_rows[0:P:32, :].rearrange("q (i c) -> q i c", c=32), in_=b_view)
         nc.sync.dma_start(out=wl_words[:].bitcast(I32), in_=ww[:, :, e_words:])
-        for r in range(4):
-            nc.sync.dma_start(out=wl_scales[:].bitcast(I32)[r:P:32], in_=ws[r, :, :, e_scales:])
+        for q in range(4):
+            nc.sync.dma_start(out=wl_scales[:].bitcast(I32)[32 * q : 32 * q + 4], in_=ws[q, :, :, e_scales:])
 
         grouped = [keep.tile([P, T, PACK], BF16, align_bytes=256, name="grouped%d" % a) for a in range(PASSES)]
         codes = [keep.tile([P, T], U32, align_bytes=256, name="codes%d" % a) for a in range(PASSES)]

@@ -77,10 +77,11 @@ def tile_mix_xres_fm_silu_kernel(tc, x4_words, x4_scales, xr, w4_words, w4_scale
             queue.dma_start(out=raw[a, t0][:], in_=xr_view[a, :, :, t0:t1])
 
         load_xr(nc.scalar, 0, 0)
-        nc.scalar.dma_start(out=wa_words[:].bitcast(I32), in_=ww[:, 0, 0:f_words])
-        nc.scalar.activation(warm_out[:], warm[:], SILU)
         for q in range(4):
-            nc.sync.dma_start(out=we_scales[:].bitcast(I32)[32 * q : 32 * q + 4], in_=ws[q, :, :, 0:e_scales])
+            queue = nc.scalar if q % 2 else nc.sync
+            queue.dma_start(out=we_scales[:].bitcast(I32)[32 * q : 32 * q + 4], in_=ws[q, :, :, 0:e_scales])
+        nc.scalar.activation(warm_out[:], warm[:], SILU)
+        nc.sync.dma_start(out=wa_words[:].bitcast(I32), in_=ww[:, 0, 0:f_words])
         load_xr(nc.sync, 0, 1)
         nc.sync.dma_start(out=wb_words[:].bitcast(I32), in_=ww[:, 0, f_words:e_words])
         load_xr(nc.sync, 0, 2)
@@ -103,15 +104,16 @@ def tile_mix_xres_fm_silu_kernel(tc, x4_words, x4_scales, xr, w4_words, w4_scale
 
         for a in range(PASSES):
             for t0, t1 in XR_STEPS[a]:
-                split = VECTOR_COLS[t1 - t0]
+                split = t1 if (a, t0) == (0, 0) else VECTOR_COLS[t1 - t0]
                 nc.vector.tensor_copy(
                     out=grouped[a][:, t0 : t0 + split, :].rearrange("p (c i) j -> p c j i", i=4),
                     in_=raw[a, t0][:, :, 0:split].rearrange("p j (c i) -> p c j i", i=4),
                 )
-                nc.scalar.copy(
-                    out=grouped[a][:, t0 + split : t1, :].rearrange("p (c i) j -> p c j i", i=4),
-                    in_=raw[a, t0][:, :, split:].rearrange("p j (c i) -> p c j i", i=4),
-                )
+                if t0 + split < t1:
+                    nc.scalar.copy(
+                        out=grouped[a][:, t0 + split : t1, :].rearrange("p (c i) j -> p c j i", i=4),
+                        in_=raw[a, t0][:, :, split:].rearrange("p j (c i) -> p c j i", i=4),
+                    )
                 nc.vector.quantize_mx(
                     out=codes[a][:, t0:t1].bitcast(FP8X4),
                     scales=scales[a][:, t0:t1],

@@ -20,9 +20,9 @@ PASSES = 2
 TILES = M // P
 BANKS = 8
 EARLY = BANKS
-BOTH = 3
+BOTH = 4
 FIRST = 4
-XR_STEPS = (((0, 128), (128, 256), (256, 384), (384, 512)), ((0, 256), (256, 512)))
+XR_STEPS = (((0, 128), (128, 256), (256, 384), (384, 512)), ((0, 256), (256, 384), (384, 512)))
 VECTOR_COLS = {128: 56, 256: 144}
 LAST = ((0, 256), (256, 384), (384, 512))
 HALF = T // 2
@@ -92,6 +92,7 @@ def tile_mix_xres_fm_silu_kernel(tc, x4_words, x4_scales, xr, w4_words, w4_scale
         load_xr(nc.sync, 1, 0)
         nc.sync.dma_start(out=w1_words[:].bitcast(I32), in_=ww[:, 1, 0:b_words])
         load_xr(nc.sync, 1, 1)
+        load_xr(nc.sync, 1, 2)
         nc.sync.dma_start(out=w2_words[:].bitcast(I32), in_=ww[:, 1, b_words:e_words])
         nc.sync.dma_start(out=b_rows[0:P:32, :].rearrange("q (i c) -> q i c", c=32), in_=b_view)
         nc.sync.dma_start(out=wl_words[:].bitcast(I32), in_=ww[:, :, e_words:])

@@ -22,6 +22,7 @@ BANKS = 8
 EARLY = BANKS
 BOTH = 4
 FIRST = 4
+PAIR = 2
 XR_STEPS = (((0, 128), (128, 256), (256, 384), (384, 512)), ((0, 256), (256, 384), (384, 512)))
 VECTOR_COLS = {128: 56, 256: 144}
 LAST = ((0, 256), (256, 384), (384, 512))
@@ -64,6 +65,7 @@ def tile_mix_xres_fm_silu_kernel(tc, x4_words, x4_scales, xr, w4_words, w4_scale
         ws = w4_scales.bitcast(I32).rearrange("a (q r) n -> q r a n", r=4)
         xr_view = xr.rearrange("(a p j) t -> a p j t", p=P, j=PACK)
         b_view = b.rearrange("(i q c) -> q i c", q=4, c=32)
+        b_dest = b_rows[0:P:32, :].rearrange("q (i c) -> q i c", c=32)
         b_words = BOTH * 2 * P // 4
         f_words = FIRST * 2 * P // 4
         e_words = EARLY * 2 * P // 4
@@ -89,12 +91,13 @@ def tile_mix_xres_fm_silu_kernel(tc, x4_words, x4_scales, xr, w4_words, w4_scale
         for q in range(4):
             nc.sync.dma_start(out=x_scales[:].bitcast(I32)[32 * q : 32 * q + 4], in_=xs[q])
         nc.sync.dma_start(out=x_words[:].bitcast(I32), in_=xw)
+        nc.sync.dma_start(out=b_dest[:, 0:BOTH], in_=b_view[:, 0:BOTH])
         load_xr(nc.sync, 1, 0)
         nc.sync.dma_start(out=w1_words[:].bitcast(I32), in_=ww[:, 1, 0:b_words])
         load_xr(nc.sync, 1, 1)
         load_xr(nc.sync, 1, 2)
         nc.sync.dma_start(out=w2_words[:].bitcast(I32), in_=ww[:, 1, b_words:e_words])
-        nc.sync.dma_start(out=b_rows[0:P:32, :].rearrange("q (i c) -> q i c", c=32), in_=b_view)
+        nc.sync.dma_start(out=b_dest[:, BOTH:], in_=b_view[:, BOTH:])
         nc.sync.dma_start(out=wl_words[:].bitcast(I32), in_=ww[:, :, e_words:])
         for q in range(4):
             nc.sync.dma_start(out=wl_scales[:].bitcast(I32)[32 * q : 32 * q + 4], in_=ws[q, :, :, e_scales:])
@@ -120,8 +123,8 @@ def tile_mix_xres_fm_silu_kernel(tc, x4_words, x4_scales, xr, w4_words, w4_scale
                     scales=scales[a][:, t0:t1],
                     in_=grouped[a][:, t0:t1, :].rearrange("p t j -> p (t j)"),
                 )
-        nc.vector.transpose(b_cols[:, 0:128], b_rows[:, 0:128])
-        nc.vector.transpose(b_cols[:, 128:384], b_rows[:, 128:384])
+            cols = slice(0, 32 * BOTH) if a == 0 else slice(32 * BOTH, 32 * TILES)
+            nc.vector.transpose(b_cols[:, cols], b_rows[:, cols])
 
         def stationary(i, a):
             if i < EARLY:
@@ -147,47 +150,67 @@ def tile_mix_xres_fm_silu_kernel(tc, x4_words, x4_scales, xr, w4_words, w4_scale
                 out=acc, lhsT=w_view, lhsT_scale=w_scale, rhs=x_view, rhs_scale=x_scale, start=start, stop=stop
             )
 
-        def open_bank(i):
-            return psum.tile([P, T], F32, name="acc%d" % i, tag="bank%d" % (i % BANKS))
+        def open_bank(name, bank):
+            return psum.tile([P, T], F32, name=name, tag="bank%d" % bank)
 
-        def finish(i, acc):
-            res = keep.tile([P, T], F32, align_bytes=256, name="res%d" % i)
-            width = HALF if i in (0, TILES - 2) else T
-            for t in range(0, T, width):
-                cols = slice(t, t + width)
-                nc.scalar.activation(res[:, cols], acc[:, cols], SILU, bias=b_cols[:, 32 * i : 32 * i + 1])
-                nc.sync.dma_start(out=out[P * i : P * (i + 1), cols], in_=res[:, cols])
+        def finish(i, acc, t0, t1):
+            res = keep.tile([P, t1 - t0], F32, align_bytes=256, name="res%d_%d" % (i, t0))
+            nc.scalar.activation(res[:], acc, SILU, bias=b_cols[:, 32 * i : 32 * i + 1])
+            nc.sync.dma_start(out=out[P * i : P * (i + 1), t0:t1], in_=res[:])
 
-        banks = [open_bank(i) for i in range(EARLY)]
+        banks = [open_bank("early%d" % n, n) for n in range(BANKS)]
+
+        def place(i, t0, t1):
+            if i >= PAIR:
+                return banks[i][:, t0:t1]
+            h = t0 // HALF
+            return banks[h][:, HALF * (i - h) + t0 : HALF * (i - h) + t1]
+
+        def pair_passes(kind, a, h, stop=False):
+            t0, t1 = HALF * h, HALF * (h + 1)
+            for i in range(PAIR):
+                multiply(place(i, t0, t1), kind, i, a, t0, t1, stop=stop and i == PAIR - 1)
+
+        def close_pair(h):
+            pair_passes("x4", 1, h)
+            pair_passes("xr", 1, h, stop=True)
+            for i in range(PAIR):
+                finish(i, place(i, HALF * h, HALF * (h + 1)), HALF * h, HALF * (h + 1))
+
         for t0, t1 in XR_STEPS[0]:
             for i in range(EARLY):
-                multiply(banks[i][:, t0:t1], "xr", i, 0, t0, t1, start=t0 == 0)
-        for i in range(EARLY):
+                opens = t0 == 0 if i >= PAIR else (i == 0 and t0 % HALF == 0)
+                multiply(place(i, t0, t1), "xr", i, 0, t0, t1, start=opens)
+        pair_passes("x4", 0, 0)
+        for i in range(PAIR, EARLY):
             multiply(banks[i][:], "x4", i, 0, 0, T)
-        for i in range(BOTH):
+        close_pair(0)
+        pair_passes("x4", 0, 1)
+        for i in range(PAIR, BOTH):
             multiply(banks[i][:], "x4", i, 1, 0, T)
-        for i in range(EARLY):
+        for i in range(PAIR, EARLY):
             if i >= BOTH:
                 multiply(banks[i][:], "x4", i, 1, 0, T)
             multiply(banks[i][:], "xr", i, 1, 0, T, stop=True)
-            finish(i, banks[i])
-        for i in range(EARLY, TILES - 1):
-            acc = open_bank(i)
+            finish(i, banks[i][:], 0, T)
+        close_pair(1)
+        for i, bank in zip(range(EARLY, TILES - 1), (0, 2, 3)):
+            acc = open_bank("late%d" % i, bank)
             for kind in ("x4", "xr"):
                 for a in range(PASSES):
                     multiply(acc[:], kind, i, a, 0, T, start=(kind, a) == ("x4", 0), stop=(kind, a) == ("xr", 1))
-            finish(i, acc)
+            width = HALF if i == TILES - 2 else T
+            for t in range(0, T, width):
+                finish(i, acc[:, t : t + width], t, t + width)
 
         i = TILES - 1
         res = keep.tile([P, T], F32, align_bytes=256, name="res_last")
         for n, (t0, t1) in enumerate(LAST):
-            acc = psum.tile([P, t1 - t0], F32, name="acc_last%d" % n, tag="bank%d" % ((i + n) % BANKS))
+            acc = psum.tile([P, t1 - t0], F32, name="acc_last%d" % n, tag="bank%d" % (4 + n))
             for a in range(PASSES):
                 multiply(acc[:], "x4", i, a, t0, t1, start=a == 0)
             for a in range(PASSES):
-                for t in range(t0, t1, P):
-                    stop = a == PASSES - 1 and t + P == t1
-                    multiply(acc[:, t - t0 : t - t0 + P], "xr", i, a, t, t + P, stop=stop)
+                multiply(acc[:], "xr", i, a, t0, t1, stop=a == PASSES - 1)
             nc.scalar.activation(res[:, t0:t1], acc[:], SILU, bias=b_cols[:, 32 * i : 32 * i + 1])
             queue = nc.scalar if t1 == T else nc.sync
             queue.dma_start(out=out[P * i : P * (i + 1), t0:t1], in_=res[:, t0:t1])

@@ -23,6 +23,7 @@ EARLY = BANKS
 BOTH = 4
 FIRST = 4
 PAIR = 2
+KINDS = ("x4", "xr")
 XR_STEPS = (((0, 128), (128, 256), (256, 384), (384, 512)), ((0, 256), (256, 384), (384, 512)))
 VECTOR_COLS = {128: 56, 256: 144}
 LAST = ((0, 256), (256, 384), (384, 512))
@@ -171,11 +172,17 @@ def tile_mix_xres_fm_silu_kernel(tc, x4_words, x4_scales, xr, w4_words, w4_scale
             for i in range(PAIR):
                 multiply(place(i, t0, t1), kind, i, a, t0, t1, stop=stop and i == PAIR - 1)
 
-        def close_pair(h):
-            pair_passes("x4", 1, h)
-            pair_passes("xr", 1, h, stop=True)
+        def close_pair(h, kinds):
+            pair_passes(kinds[0], 1, h)
+            pair_passes(kinds[1], 1, h, stop=True)
             for i in range(PAIR):
                 finish(i, place(i, HALF * h, HALF * (h + 1)), HALF * h, HALF * (h + 1))
+
+        def whole_sum(acc, i, t0, t1, kinds):
+            for kind in kinds:
+                for a in range(PASSES):
+                    first, last = (kind, a) == (kinds[0], 0), (kind, a) == (kinds[1], PASSES - 1)
+                    multiply(acc, kind, i, a, t0, t1, start=first, stop=last)
 
         for t0, t1 in XR_STEPS[0]:
             for i in range(EARLY):
@@ -184,21 +191,19 @@ def tile_mix_xres_fm_silu_kernel(tc, x4_words, x4_scales, xr, w4_words, w4_scale
         pair_passes("x4", 0, 0)
         for i in range(PAIR, EARLY):
             multiply(banks[i][:], "x4", i, 0, 0, T)
-        close_pair(0)
+        close_pair(0, KINDS)
         pair_passes("x4", 0, 1)
         for i in range(PAIR, BOTH):
             multiply(banks[i][:], "x4", i, 1, 0, T)
         for i in range(PAIR, EARLY):
-            if i >= BOTH:
-                multiply(banks[i][:], "x4", i, 1, 0, T)
-            multiply(banks[i][:], "xr", i, 1, 0, T, stop=True)
+            kinds = ("xr",) if i < BOTH else KINDS if i % 2 else KINDS[::-1]
+            for kind in kinds:
+                multiply(banks[i][:], kind, i, 1, 0, T, stop=kind == kinds[-1])
             finish(i, banks[i][:], 0, T)
-        close_pair(1)
+        close_pair(1, KINDS[::-1])
         for i, bank in zip(range(EARLY, TILES - 1), (0, 2, 3)):
             acc = open_bank("late%d" % i, bank)
-            for kind in ("x4", "xr"):
-                for a in range(PASSES):
-                    multiply(acc[:], kind, i, a, 0, T, start=(kind, a) == ("x4", 0), stop=(kind, a) == ("xr", 1))
+            whole_sum(acc[:], i, 0, T, KINDS[::-1] if i % 2 else KINDS)
             width = HALF if i == TILES - 2 else T
             for t in range(0, T, width):
                 finish(i, acc[:, t : t + width], t, t + width)
@@ -207,10 +212,7 @@ def tile_mix_xres_fm_silu_kernel(tc, x4_words, x4_scales, xr, w4_words, w4_scale
         res = keep.tile([P, T], F32, align_bytes=256, name="res_last")
         for n, (t0, t1) in enumerate(LAST):
             acc = psum.tile([P, t1 - t0], F32, name="acc_last%d" % n, tag="bank%d" % (4 + n))
-            for a in range(PASSES):
-                multiply(acc[:], "x4", i, a, t0, t1, start=a == 0)
-            for a in range(PASSES):
-                multiply(acc[:], "xr", i, a, t0, t1, stop=a == PASSES - 1)
+            whole_sum(acc[:], i, t0, t1, KINDS if n % 2 else KINDS[::-1])
             nc.scalar.activation(res[:, t0:t1], acc[:], SILU, bias=b_cols[:, 32 * i : 32 * i + 1])
             queue = nc.scalar if t1 == T else nc.sync
             queue.dma_start(out=out[P * i : P * (i + 1), t0:t1], in_=res[:, t0:t1])

from contextlib import ExitStack

import concourse.mybir as mybir

K, M, T = 1024, 1536, 512
FLOPS = 2 * 2 * K * M * T

F32 = mybir.dt.float32
BF16 = mybir.dt.bfloat16
I32 = mybir.dt.int32
U32 = mybir.dt.uint32
U8 = mybir.dt.uint8
FP8X4 = mybir.dt.float8_e4m3fn_x4
FP4X4 = mybir.dt.float4_e2m1fn_x4
SILU = mybir.ActivationFunctionType.Silu

P = 128
PACK = 4
PASSES = 2
TILES = M // P
BANKS = 8
EARLY = BANKS
BOTH = 4
FIRST = 4
PAIR = 2
KINDS = ("x4", "xr")
XR_STEPS = (((0, 128), (128, 256), (256, 384), (384, 512)), ((0, 256), (256, 384), (384, 512)))
VECTOR_COLS = {128: 56, 256: 144}
LAST = ((0, 256), (256, 384), (384, 512))
HALF = T // 2


def tile_mix_xres_fm_silu_kernel(tc, x4_words, x4_scales, xr, w4_words, w4_scales, b, out):
    nc = tc.nc
    with ExitStack() as ctx:
        keep = ctx.enter_context(tc.tile_pool(name="keep", bufs=1))
        psum = ctx.enter_context(tc.psum_pool(name="psum", bufs=1))
        ctx.enter_context(tc.manual_schedule())

        def byte_tile(name, *shape):
            return keep.tile([P, *shape], U8, align_bytes=256, name=name)

        x_words = byte_tile("x_words", PASSES, 2 * T)
        x_scales = byte_tile("x_scales", PASSES, T)
        wa_words = byte_tile("wa_words", FIRST * 2 * P)
        wb_words = byte_tile("wb_words", (EARLY - FIRST) * 2 * P)
        w1_words = byte_tile("w1_words", BOTH * 2 * P)
        w2_words = byte_tile("w2_words", (EARLY - BOTH) * 2 * P)
        we_scales = byte_tile("we_scales", PASSES, EARLY * P)
        wl_words = byte_tile("wl_words", PASSES, (TILES - EARLY) * 2 * P)
        wl_scales = byte_tile("wl_scales", PASSES, (TILES - EARLY) * P)
        warm = keep.tile([P, 1], F32)
        warm_out = keep.tile([P, 1], F32)
        b_rows = keep.tile([P, TILES * 32], F32, align_bytes=64)
        b_cols = keep.tile([P, TILES * 32], F32, align_bytes=64)

        nc.vector.memset(we_scales[:].bitcast(I32), 0)
        nc.vector.memset(warm[:], 0.0)
        nc.vector.memset(x_scales[:].bitcast(I32), 0)
        nc.vector.memset(b_rows[:], 0.0)
        nc.vector.memset(wl_scales[:].bitcast(I32), 0)

        xw = x4_words.bitcast(I32).rearrange("a p n -> p a n")
        ww = w4_words.bitcast(I32).rearrange("a p n -> p a n")
        xs = x4_scales.bitcast(I32).rearrange("a (q r) n -> q r a n", r=4)
        ws = w4_scales.bitcast(I32).rearrange("a (q r) n -> q r a n", r=4)
        xr_view = xr.rearrange("(a p j) t -> a p j t", p=P, j=PACK)
        b_view = b.rearrange("(i q c) -> q i c", q=4, c=32)
        b_dest = b_rows[0:P:32, :].rearrange("q (i c) -> q i c", c=32)
        b_words = BOTH * 2 * P // 4
        f_words = FIRST * 2 * P // 4
        e_words = EARLY * 2 * P // 4
        e_scales = EARLY * P // 4

        raw = {}

        def load_xr(queue, a, n):
            t0, t1 = XR_STEPS[a][n]
            raw[a, t0] = keep.tile([P, PACK, t1 - t0], F32, align_bytes=256, name="raw%d_%d" % (a, n))
            queue.dma_start(out=raw[a, t0][:], in_=xr_view[a, :, :, t0:t1])

        load_xr(nc.scalar, 0, 0)
        for q in range(4):
            queue = nc.scalar if q % 2 else nc.sync
            queue.dma_start(out=we_scales[:].bitcast(I32)[32 * q : 32 * q + 4], in_=ws[q, :, :, 0:e_scales])
        nc.scalar.activation(warm_out[:], warm[:], SILU)
        nc.sync.dma_start(out=wa_words[:].bitcast(I32), in_=ww[:, 0, 0:f_words])
        load_xr(nc.sync, 0, 1)
        nc.sync.dma_start(out=wb_words[:].bitcast(I32), in_=ww[:, 0, f_words:e_words])
        load_xr(nc.sync, 0, 2)
        load_xr(nc.sync, 0, 3)
        for q in range(4):
            nc.sync.dma_start(out=x_scales[:].bitcast(I32)[32 * q : 32 * q + 4], in_=xs[q])
        nc.sync.dma_start(out=x_words[:].bitcast(I32), in_=xw)
        nc.sync.dma_start(out=b_dest[:, 0:BOTH], in_=b_view[:, 0:BOTH])
        load_xr(nc.sync, 1, 0)
        nc.sync.dma_start(out=w1_words[:].bitcast(I32), in_=ww[:, 1, 0:b_words])
        load_xr(nc.sync, 1, 1)
        load_xr(nc.sync, 1, 2)
        nc.sync.dma_start(out=w2_words[:].bitcast(I32), in_=ww[:, 1, b_words:e_words])
        nc.sync.dma_start(out=b_dest[:, BOTH:], in_=b_view[:, BOTH:])
        nc.sync.dma_start(out=wl_words[:].bitcast(I32), in_=ww[:, :, e_words:])
        for q in range(4):
            nc.sync.dma_start(out=wl_scales[:].bitcast(I32)[32 * q : 32 * q + 4], in_=ws[q, :, :, e_scales:])

        grouped = [keep.tile([P, T, PACK], BF16, align_bytes=256, name="grouped%d" % a) for a in range(PASSES)]
        codes = [keep.tile([P, T], U32, align_bytes=256, name="codes%d" % a) for a in range(PASSES)]
        scales = [keep.tile([P, T], U8, align_bytes=256, name="scales%d" % a) for a in range(PASSES)]

        for a in range(PASSES):
            for t0, t1 in XR_STEPS[a]:
                split = t1 if (a, t0) == (0, 0) else VECTOR_COLS[t1 - t0]
                nc.vector.tensor_copy(
                    out=grouped[a][:, t0 : t0 + split, :].rearrange("p (c i) j -> p c j i", i=4),
                    in_=raw[a, t0][:, :, 0:split].rearrange("p j (c i) -> p c j i", i=4),
                )
                if t0 + split < t1:
                    nc.scalar.copy(
                        out=grouped[a][:, t0 + split : t1, :].rearrange("p (c i) j -> p c j i", i=4),
                        in_=raw[a, t0][:, :, split:].rearrange("p j (c i) -> p c j i", i=4),
                    )
                nc.vector.quantize_mx(
                    out=codes[a][:, t0:t1].bitcast(FP8X4),
                    scales=scales[a][:, t0:t1],
                    in_=grouped[a][:, t0:t1, :].rearrange("p t j -> p (t j)"),
                )
            cols = slice(0, 32 * BOTH) if a == 0 else slice(32 * BOTH, 32 * TILES)
            nc.vector.transpose(b_cols[:, cols], b_rows[:, cols])

        def stationary(i, a):
            if i < EARLY:
                cut, below, above = (FIRST, wa_words, wb_words) if a == 0 else (BOTH, w1_words, w2_words)
                words, k = (below, i) if i < cut else (above, i - cut)
                return (
                    words[:, 2 * P * k : 2 * P * (k + 1)].bitcast(FP4X4),
                    we_scales[:, a, P * i : P * (i + 1)],
                )
            k = i - EARLY
            return (
                wl_words[:, a, 2 * P * k : 2 * P * (k + 1)].bitcast(FP4X4),
                wl_scales[:, a, P * k : P * (k + 1)],
            )

        def multiply(acc, kind, i, a, t0, t1, start=False, stop=False):
            w_view, w_scale = stationary(i, a)
            if kind == "x4":
                x_view, x_scale = x_words[:, a, 2 * t0 : 2 * t1].bitcast(FP4X4), x_scales[:, a, t0:t1]
            else:
                x_view, x_scale = codes[a][:, t0:t1].bitcast(FP8X4), scales[a][:, t0:t1]
            nc.tensor.matmul_mx(
                out=acc, lhsT=w_view, lhsT_scale=w_scale, rhs=x_view, rhs_scale=x_scale, start=start, stop=stop
            )

        def open_bank(name, bank):
            return psum.tile([P, T], F32, name=name, tag="bank%d" % bank)

        def finish(i, acc, t0, t1):
            res = keep.tile([P, t1 - t0], F32, align_bytes=256, name="res%d_%d" % (i, t0))
            nc.scalar.activation(res[:], acc, SILU, bias=b_cols[:, 32 * i : 32 * i + 1])
            nc.sync.dma_start(out=out[P * i : P * (i + 1), t0:t1], in_=res[:])

        banks = [open_bank("early%d" % n, n) for n in range(BANKS)]

        def place(i, t0, t1):
            if i >= PAIR:
                return banks[i][:, t0:t1]
            h = t0 // HALF
            return banks[h][:, HALF * (i - h) + t0 : HALF * (i - h) + t1]

        def pair_passes(kind, a, h, stop=False):
            t0, t1 = HALF * h, HALF * (h + 1)
            for i in range(PAIR):
                multiply(place(i, t0, t1), kind, i, a, t0, t1, stop=stop and i == PAIR - 1)

        def close_pair(h, kinds):
            pair_passes(kinds[0], 1, h)
            pair_passes(kinds[1], 1, h, stop=True)
            for i in range(PAIR):
                finish(i, place(i, HALF * h, HALF * (h + 1)), HALF * h, HALF * (h + 1))

        def whole_sum(acc, i, t0, t1, kinds):
            for kind in kinds:
                for a in range(PASSES):
                    first, last = (kind, a) == (kinds[0], 0), (kind, a) == (kinds[1], PASSES - 1)
                    multiply(acc, kind, i, a, t0, t1, start=first, stop=last)

        for t0, t1 in XR_STEPS[0]:
            for i in range(EARLY):
                opens = t0 == 0 if i >= PAIR else (i == 0 and t0 % HALF == 0)
                multiply(place(i, t0, t1), "xr", i, 0, t0, t1, start=opens)
        pair_passes("x4", 0, 0)
        for i in range(PAIR, EARLY):
            multiply(banks[i][:], "x4", i, 0, 0, T)
        close_pair(0, KINDS)
        pair_passes("x4", 0, 1)
        for i in range(PAIR, BOTH):
            multiply(banks[i][:], "x4", i, 1, 0, T)
        for i in range(PAIR, EARLY):
            kinds = ("xr",) if i < BOTH else KINDS if i % 2 else KINDS[::-1]
            for kind in kinds:
                multiply(banks[i][:], kind, i, 1, 0, T, stop=kind == kinds[-1])
            finish(i, banks[i][:], 0, T)
        close_pair(1, KINDS[::-1])
        for i, bank in zip(range(EARLY, TILES - 1), (0, 2, 3)):
            acc = open_bank("late%d" % i, bank)
            whole_sum(acc[:], i, 0, T, KINDS[::-1] if i % 2 else KINDS)
            width = HALF if i == TILES - 2 else T
            for t in range(0, T, width):
                finish(i, acc[:, t : t + width], t, t + width)

        i = TILES - 1
        res = keep.tile([P, T], F32, align_bytes=256, name="res_last")
        for n, (t0, t1) in enumerate(LAST):
            acc = psum.tile([P, t1 - t0], F32, name="acc_last%d" % n, tag="bank%d" % (4 + n))
            whole_sum(acc[:], i, t0, t1, KINDS if n % 2 else KINDS[::-1])
            nc.scalar.activation(res[:, t0:t1], acc[:], SILU, bias=b_cols[:, 32 * i : 32 * i + 1])
            queue = nc.scalar if t1 == T else nc.sync
            queue.dma_start(out=out[P * i : P * (i + 1), t0:t1], in_=res[:, t0:t1])
